import numpy as np
import ml_dtypes


def mxq(x, axis, fmt="e4m3"):
    dtype, down = {"e4m3": (ml_dtypes.float8_e4m3fn, 7), "e5m2": (ml_dtypes.float8_e5m2, 14)}[fmt]
    v = np.moveaxis(np.asarray(x, np.float32).astype(ml_dtypes.bfloat16).astype(np.float64), axis, -1)
    blocks = v.reshape(v.shape[:-1] + (-1, 32))
    amax = np.abs(blocks).max(-1, keepdims=True)
    byte = np.maximum(np.where(amax > 0, np.frexp(amax)[1] - 1 + 127, 0) - down, 1)
    scale = np.exp2(byte - 127.0)
    codes = (blocks / scale).astype(np.float32).astype(dtype).astype(np.float64)
    return np.moveaxis((codes * scale).reshape(v.shape), -1, axis)


WIDE = False


def mx_kscale(k):
    if not WIDE:
        return np.ones(k)
    levels = np.array([10, -10, 5, -5, 0])
    if k % 512:
        return np.exp2(np.random.permutation(np.resize(levels, k // 32))).repeat(32)
    a = np.empty((k // 512, 16))
    for p in range(k // 512):
        a[p, :8] = np.random.permutation(np.resize(levels, 8))
        for g in range(8):
            far = levels[np.abs(levels - a[p, g]) >= 10]
            a[p, g + 8] = far[np.random.randint(len(far))]
    return np.exp2(a.ravel()).repeat(32)


def f64(x):
    return np.asarray(x).astype(np.float64)


def striped(idx):
    return np.tile(idx.reshape(-1, 16).T, (8, 1)).astype(np.uint16)


def unstriped(offs):
    return offs[:16].T.reshape(-1).astype(np.int64)


E2M1 = np.array([0.0, 0.5, 1.0, 1.5, 2.0, 3.0, 4.0, 6.0, -0.0, -0.5, -1.0, -1.5, -2.0, -3.0, -4.0, -6.0])


def pack_weight(w, fmt):
    k, n = w.shape
    w = f64(np.asarray(w, np.float32).astype(ml_dtypes.bfloat16)).reshape(k // 32, 32, n)
    amax = np.abs(w).max(1)
    if fmt == "e4m3":
        byte = np.frexp(amax)[1] - 1 + 127 - 7
    else:
        mant, ex = np.frexp(amax / 6.0)
        byte = np.where(mant > 0.5, ex, ex - 1) + 127
    byte = np.clip(np.where(amax > 0, byte, 1), 1, 254)
    scaled = (w * np.exp2(127.0 - byte)[:, None, :]).reshape(k, n).astype(np.float32)
    by_word = np.ascontiguousarray(scaled.reshape(k // 512, 128, 4, n).transpose(0, 1, 3, 2))
    if fmt == "e4m3":
        words = by_word.astype(ml_dtypes.float8_e4m3fn).view(np.uint8)
    else:
        c = by_word.astype(ml_dtypes.float4_e2m1fn).view(np.uint8) & 0xF
        words = (c[..., 0::2] | (c[..., 1::2] << 4)).reshape(k // 512, 128, 2 * n)
    return np.ascontiguousarray(words), np.ascontiguousarray(byte.astype(np.uint8).reshape(k // 512, 16, n))


def unpack_weight(words, scales, fmt):
    g, _, n = scales.shape
    words = np.ascontiguousarray(words).reshape(g, 128, n, -1)
    if fmt == "e4m3":
        vals = words.view(ml_dtypes.float8_e4m3fn).astype(np.float64)
    else:
        nib = np.empty((g, 128, n, 4), np.uint8)
        nib[..., 0::2] = words & 0xF
        nib[..., 1::2] = words >> 4
        vals = E2M1[nib]
    vals = vals * np.repeat(np.exp2(scales.astype(np.float64) - 127.0), 8, axis=1)[..., None]
    return vals.transpose(0, 1, 3, 2).reshape(g * 512, n)


K, T, E, C, H, N = 256, 512, 4, 256, 512, 1536


def by_expert(wq, xq):
    return np.concatenate([wq[e].T @ xq[:, e * C:(e + 1) * C] for e in range(E)], axis=1)


def setup_inputs():
    n = np.random.standard_normal
    v = mx_kscale(N)
    u = mx_kscale(H)
    first = np.random.permutation(np.repeat(np.arange(E), T // E))
    second = (first + 1 + np.random.permutation(np.repeat(np.arange(E - 1), -(-T // (E - 1)))[:T])) % E
    while np.bincount(second, minlength=E).max() != T // E:
        load = np.bincount(second, minlength=E); hi, lo = int(load.argmax()), int(load.argmin())
        t = np.flatnonzero((second == hi) & (first != lo))[0]; second[t] = lo
    slot_token = np.empty(E * C, np.int64); pos = np.empty((2, T), np.int64); fill = np.zeros(E, np.int64)
    place = np.stack([np.random.permutation(C) for _ in range(E)])
    for r, deal in enumerate((first, second)):
        for t in np.random.permutation(T):
            e = deal[t]; j = e * C + place[e, fill[e]]; fill[e] += 1; slot_token[j] = t; pos[r, t] = j
    g = np.random.uniform(0.2, 0.8, T)
    w_slot = np.empty(E * C); w_slot[pos[0]] = g; w_slot[pos[1]] = 1.0 - g
    dy = pack_weight(n((N, T)) * v[:, None], "e4m3")
    wt = pack_weight(n((N, K)) / np.sqrt(N) / v[:, None], "e4m3")
    wbt = [pack_weight(m, "e4m3") for m in n((E, N, H)) / np.sqrt(N) / v[None, :, None] * u]
    wat = [pack_weight(m, "e4m3") for m in n((E, H, K)) / np.sqrt(H) / u[None, :, None]]
    return {
        "dy_words": dy[0],
        "dy_scales": dy[1],
        "wt_words": wt[0],
        "wt_scales": wt[1],
        "wbt_words": np.stack([m[0] for m in wbt]),
        "wbt_scales": np.stack([m[1] for m in wbt]),
        "wat_words": np.stack([m[0] for m in wat]),
        "wat_scales": np.stack([m[1] for m in wat]),
        "gate": (np.tile(w_slot, (128, 1))).astype(np.float32),
        "offs": striped(slot_token),
        "pos1": striped(pos[0]),
        "pos2": striped(pos[1]),
    }


def reference(dy_words, dy_scales, wt_words, wt_scales, wbt_words, wbt_scales, wat_words, wat_scales, gate, offs, pos1, pos2):
    wt = unpack_weight(wt_words, wt_scales, "e4m3")
    wbt = np.stack([unpack_weight(wbt_words[e], wbt_scales[e], "e4m3") for e in range(E)])
    wat = np.stack([unpack_weight(wat_words[e], wat_scales[e], "e4m3") for e in range(E)])
    idx = unstriped(offs)
    dy = unpack_weight(dy_words, dy_scales, "e4m3")
    base = wt.T @ dy
    dh = f64(gate[:1]) * by_expert(wbt, dy[:, idx])
    dx = by_expert(wat, mxq(dh, 0, "e4m3"))
    c = dx[:, unstriped(pos1)] + dx[:, unstriped(pos2)]
    return base + c

@@ -1,0 +1,220 @@
+from contextlib import ExitStack
+
+import concourse.mybir as mybir
+from concourse.masks import make_identity
+
+K, T, E, C, H, N = 256, 512, 4, 256, 512, 1536
+S = E * C
+P = 128
+PASSES = N // 512
+FLOPS = 2 * N * K * T + 2 * N * H * S + 2 * H * K * S
+
+F32 = mybir.dt.float32
+BF16 = mybir.dt.bfloat16
+I32 = mybir.dt.int32
+U32 = mybir.dt.uint32
+U16 = mybir.dt.uint16
+U8 = mybir.dt.uint8
+X4 = mybir.dt.float8_e4m3fn_x4
+COPY = mybir.ActivationFunctionType.Copy
+ADD = mybir.AluOpType.add
+
+BYTE_GATHERS = [(0, 128), (128, 128), (256, 256), (512, 256), (768, 256)]
+AHEAD = 3
+UNITS = [(0, 256), (256, 256), (512, 256), (768, 128), (896, 128)]
+DX_ON_VECTOR = (0, 1)
+PIECE = 256
+
+
+def tile_moe_adb_none_kernel(
+    tc, dy_words, dy_scales, wt_words, wt_scales, wbt_words, wbt_scales, wat_words, wat_scales,
+    gate, offs, pos1, pos2, out,
+):
+    nc = tc.nc
+    with ExitStack() as ctx:
+        keep = ctx.enter_context(tc.tile_pool(name="keep", bufs=1))
+        psum = ctx.enter_context(tc.psum_pool(name="psum", bufs=1))
+
+        def sb(name, shape, dtype, slot=None):
+            return keep.tile(shape, dtype, name=name, tag=slot or name, align_bytes=64)
+
+        offs_sb = keep.tile([P, S // 16], U16, name="offs_sb")
+        pos_sb = [keep.tile([P, T // 16], U16, name="pos%d_sb" % r) for r in range(2)]
+
+        dy_first = sb("dy_first", [P, T], U32)
+        dy_rest = sb("dy_rest", [P, PASSES - 1, T], U32)
+        dy_w = [dy_first[:]] + [dy_rest[:, s, :] for s in range(PASSES - 1)]
+        dy_s = sb("dy_s", [P, T], U8)
+        wb_s = sb("wb_s", [P, E * PASSES, H], U8)
+        gate_rows = sb("gate_rows", [P, P], F32, "slot_words")
+        gate_cols = sb("gate_cols", [P, S // P], F32)
+        ident = sb("ident", [P, P], F32)
+
+        nc.gpsimd.memset(dy_s[:].bitcast(I32), 0)
+        nc.vector.memset(wb_s[:].bitcast(I32), 0)
+
+        dy_hbm = dy_words.rearrange("s p t d -> p s (t d)").bitcast(I32)
+        wa_hbm = wat_words.rearrange("e s p k d -> p (e s) (k d)").bitcast(I32)
+        wt_hbm = wt_words.rearrange("s p k d -> p s (k d)").bitcast(I32)
+        dys_hbm = dy_scales.bitcast(I32)
+        wbs_hbm = wbt_scales.bitcast(I32).rearrange("e s b i -> b (e s) i")
+        was_hbm = wat_scales.bitcast(I32).rearrange("e s b k -> b (e s) k")
+        wts_hbm = wt_scales.bitcast(I32).rearrange("s b k -> b s k")
+
+        def load_dy_scales(queue, q):
+            queue.dma_start(out=dy_s[32 * q:32 * q + 4 * PASSES, :].bitcast(I32), in_=dys_hbm[:, 4 * q:4 * q + 4, :])
+
+        def load_scales(queue, tile, row0, hbm):
+            for q in range(4):
+                queue.dma_start(out=tile[32 * q + row0:32 * q + row0 + 4, :, :].bitcast(I32), in_=hbm[4 * q:4 * q + 4])
+
+        WB_ROW = 0
+        WT_ROW = 8
+        WA_ROW = 12
+
+        nc.sync.dma_start(offs_sb[:], offs)
+        nc.sync.dma_start(out=dy_first[:].bitcast(I32), in_=dy_hbm[:, 0, :])
+        nc.scalar.dma_start(out=gate_rows[:], in_=gate.rearrange("r (c p) -> (r c) p", p=P)[0:P, :])
+        nc.sync.dma_start(pos_sb[0][:], pos1)
+        nc.sync.dma_start(pos_sb[1][:], pos2)
+        nc.sync.dma_start(out=dy_rest[:].bitcast(I32), in_=dy_hbm[:, 1:PASSES, :])
+        wb_all = wbt_words.rearrange("e s p i d -> p (e s) (i d)").bitcast(I32)
+        wb_first = sb("wb_first", [P, H], U32)
+        nc.sync.dma_start(out=wb_first[:].bitcast(I32), in_=wb_all[:, 0, :])
+        make_identity(nc, ident[:])
+        load_dy_scales(nc.scalar, 0)
+        load_dy_scales(nc.scalar, 1)
+        load_dy_scales(nc.sync, 2)
+        load_dy_scales(nc.sync, 3)
+        load_scales(nc.sync, wb_s, WB_ROW, wbs_hbm)
+
+        turned = psum.tile([P, 4, P], F32, name="turned", tag="turned", bufs=2)
+        nc.tensor.transpose(turned[:, 0, :], gate_rows[:], ident[:])
+        nc.scalar.activation(gate_cols[:], turned[:, 0, 0:S // P], COPY)
+
+        wb_cols = (E * PASSES - 1) * H
+        later = sb("later", [P, wb_cols + E * K + PASSES * K], U32, "slot_words")
+        wb_next = later[:, 0:wb_cols].rearrange("p (a i) -> p a i", i=H)
+        wa_w = later[:, wb_cols:wb_cols + E * K].rearrange("p (e k) -> p e k", k=K)
+        wt_w = later[:, wb_cols + E * K:].rearrange("p (s k) -> p s k", k=K)
+        for e in range(E):
+            a0 = max(e * PASSES, 1)
+            nc.sync.dma_start(out=wb_next[:, a0 - 1:(e + 1) * PASSES - 1, :].bitcast(I32), in_=wb_all[:, a0:(e + 1) * PASSES, :])
+        nc.sync.dma_start(out=wa_w.bitcast(I32), in_=wa_hbm)
+        nc.sync.dma_start(out=wt_w.bitcast(I32), in_=wt_hbm)
+        wb_w = [wb_first[:]] + [wb_next[:, a, :] for a in range(E * PASSES - 1)]
+
+        g_s = {}
+
+        def gather_bytes(j0, size):
+            scales = sb("g_s%d" % j0, [P, size], U8, {0: "slot_was", P: "slot_wts"}.get(j0))
+            nc.vector.tensor_copy(scales[:], dy_s[:].indirect(offs_sb[:, j0 // 16:(j0 + size) // 16]))
+            for j in range(j0, j0 + size, P):
+                g_s[j] = (scales, j - j0)
+
+        def gather_words(j):
+            words = []
+            for s in range(PASSES):
+                tile = keep.tile([P, P], U32, name="g_w%d" % s, tag="g_w%d" % s, bufs=AHEAD, align_bytes=64)
+                nc.vector.tensor_copy(tile[:], dy_w[s].indirect(offs_sb[:, j // 16:(j + P) // 16]))
+                words.append(tile)
+            return words
+
+        def stage1(j):
+            e = j // C
+            if j in dict(BYTE_GATHERS):
+                gather_bytes(j, dict(BYTE_GATHERS)[j])
+            words = gather_words(j)
+            scales, c0 = g_s[j]
+            acc = psum.tile([P, H], F32, name="acc1", tag="acc", bufs=5)
+            for s in range(PASSES):
+                nc.tensor.matmul_mx(
+                    out=acc[:],
+                    lhsT=words[s][:].bitcast(X4),
+                    lhsT_scale=scales[4 * s:P, c0:c0 + P],
+                    rhs=wb_w[e * PASSES + s].bitcast(X4),
+                    rhs_scale=wb_s[WB_ROW:P, e * PASSES + s, :],
+                    start=(s == 0), stop=(s == PASSES - 1),
+                )
+            dh = sb("dh%d" % (j // P), [P, 2, P, 2], BF16)
+            nc.scalar.activation(dh[:], acc[:].rearrange("j (p u v) -> j u p v", u=2, v=2), COPY,
+                                 scale=gate_cols[:, j // P:j // P + 1])
+            return dh
+
+        def turn(n, j0, size, dhs):
+            bank = psum.tile([P, 4, P], F32, name="turned", tag="turned", bufs=2)
+            for m, dh in enumerate(dhs):
+                pairs = dh[:].rearrange("j u p v -> j (u p v)").bitcast(F32)
+                for u in range(2):
+                    nc.tensor.transpose(bank[:, 2 * m + u, :], pairs[:, u * P:(u + 1) * P], ident[:])
+            dht = sb("dht%d" % n, [P, size // P, P, 2], F32)
+            nc.scalar.copy(dht[:], bank[:, 0:2 * len(dhs), :].rearrange("p (m u) j -> p m j u", u=2))
+            return dht
+
+        dhts = []
+        for n, (j0, size) in enumerate(UNITS):
+            dhs = [stage1(j) for j in range(j0, j0 + size, P)]
+            dhts.append(turn(n, j0, size, dhs))
+            if n == 0:
+                wa_s = sb("wa_s", [P, E, K], U8, "slot_was")
+                nc.gpsimd.memset(wa_s[:].bitcast(I32), 0)
+                load_scales(nc.sync, wa_s, WA_ROW, was_hbm)
+                wt_s = sb("wt_s", [P, PASSES, K], U8, "slot_wts")
+                nc.gpsimd.memset(wt_s[:].bitcast(I32), 0)
+                load_scales(nc.sync, wt_s, WT_ROW, wts_hbm)
+
+        dx = sb("dx", [P, 2, S], F32)
+        for n, (j0, size) in enumerate(UNITS):
+            e = j0 // C
+            codes = sb("dh_w%d" % n, [P, size], U32)
+            plane = sb("dh_s%d" % n, [P, size], U8)
+            nc.vector.quantize_mx(out=codes[:].bitcast(X4), scales=plane[:],
+                                  in_=dhts[n][:].rearrange("p m j u -> p (m j u)").bitcast(BF16))
+            acc = psum.tile([P, 2, C], F32, name="acc2", tag="acc", bufs=5)
+            for h in range(2):
+                nc.tensor.matmul_mx(
+                    out=acc[:, h, 0:size],
+                    lhsT=wa_w[:, e, h * P:(h + 1) * P].bitcast(X4),
+                    lhsT_scale=wa_s[WA_ROW:P, e, h * P:(h + 1) * P],
+                    rhs=codes[:].bitcast(X4), rhs_scale=plane[:],
+                    start=True, stop=True,
+                )
+            if n in DX_ON_VECTOR:
+                nc.vector.tensor_copy(dx[:, :, j0:j0 + size], acc[:, :, 0:size])
+            else:
+                nc.scalar.copy(dx[:, :, j0:j0 + size], acc[:, :, 0:size])
+
+        base = []
+        for h in range(2):
+            acc = psum.tile([P, T], F32, name="base%d" % h, tag="acc", bufs=5)
+            for s in range(PASSES):
+                nc.tensor.matmul_mx(
+                    out=acc[:],
+                    lhsT=wt_w[:, s, h * P:(h + 1) * P].bitcast(X4),
+                    lhsT_scale=wt_s[WT_ROW:P, s, h * P:(h + 1) * P],
+                    rhs=dy_w[s].bitcast(X4), rhs_scale=dy_s[4 * s:P, :],
+                    start=(s == 0), stop=(s == PASSES - 1),
+                )
+            base.append(acc)
+
+        pending = None
+        for h in range(2):
+            for t0 in range(0, T, PIECE):
+                cols = slice(t0 // 16, (t0 + PIECE) // 16)
+                tag = "%d_%d" % (h, t0)
+                first = sb("first" + tag, [P, PIECE], F32)
+                second = sb("second" + tag, [P, PIECE], F32)
+                part = sb("part" + tag, [P, PIECE], F32)
+                total = sb("total" + tag, [P, PIECE], F32)
+                nc.vector.tensor_copy(first[:], dx[:, h, :].indirect(pos_sb[0][:, cols]))
+                if pending is not None:
+                    pending()
+                nc.vector.tensor_copy(second[:], dx[:, h, :].indirect(pos_sb[1][:, cols]))
+                nc.vector.tensor_tensor(part[:], base[h][:, t0:t0 + PIECE], first[:], ADD)
+
+                def finish(h=h, t0=t0, part=part, second=second, total=total):
+                    nc.vector.tensor_tensor(total[:], part[:], second[:], ADD)
+                    nc.sync.dma_start(out=out[h * P:(h + 1) * P, t0:t0 + PIECE], in_=total[:])
+
+                pending = finish
+        pending()

@@ -18,12 +18,17 @@ U8 = mybir.dt.uint8
 X4 = mybir.dt.float8_e4m3fn_x4
 COPY = mybir.ActivationFunctionType.Copy
 ADD = mybir.AluOpType.add
+MULT = mybir.AluOpType.mult
 
-BYTE_GATHERS = [(0, 128), (128, 128), (256, 256), (512, 256), (768, 256)]
-AHEAD = 3
+BYTE_GATHERS = {0: 128, 128: 128, 256: 256, 512: 256, 768: 256}
+WORD_GATHERS = {0: 128, 128: 128, 256: 256, 512: 256, 768: 128, 896: 128}
+EARLY_WORDS = {(0, 0): "late_words", (0, 1): None, (0, 2): None,
+               (128, 0): "frozen_loads", (128, 1): None, (128, 2): None, (256, 0): None}
+DX_ON_VECTOR = (0, 1, 2)
+DX_BANKS = (4, 5, 4, 3)
+PIECES = [(0, 0, 256), (0, 256, 256), (1, 0, 128), (1, 128, 256), (1, 384, 128)]
+ON_TENSOR = 3
 UNITS = [(0, 256), (256, 256), (512, 256), (768, 128), (896, 128)]
-DX_ON_VECTOR = (0, 1)
-PIECE = 256
 
 
 def tile_moe_adb_none_kernel(
@@ -73,18 +78,16 @@ def tile_moe_adb_none_kernel(
         WA_ROW = 12
 
         nc.sync.dma_start(offs_sb[:], offs)
-        nc.sync.dma_start(out=dy_first[:].bitcast(I32), in_=dy_hbm[:, 0, :])
         nc.scalar.dma_start(out=gate_rows[:], in_=gate.rearrange("r (c p) -> (r c) p", p=P)[0:P, :])
         nc.sync.dma_start(pos_sb[0][:], pos1)
         nc.sync.dma_start(pos_sb[1][:], pos2)
+        nc.sync.dma_start(out=dy_first[:].bitcast(I32), in_=dy_hbm[:, 0, :])
         nc.sync.dma_start(out=dy_rest[:].bitcast(I32), in_=dy_hbm[:, 1:PASSES, :])
         wb_all = wbt_words.rearrange("e s p i d -> p (e s) (i d)").bitcast(I32)
-        wb_first = sb("wb_first", [P, H], U32)
-        nc.sync.dma_start(out=wb_first[:].bitcast(I32), in_=wb_all[:, 0, :])
         make_identity(nc, ident[:])
         load_dy_scales(nc.scalar, 0)
         load_dy_scales(nc.scalar, 1)
-        load_dy_scales(nc.sync, 2)
+        load_dy_scales(nc.scalar, 2)
         load_dy_scales(nc.sync, 3)
         load_scales(nc.sync, wb_s, WB_ROW, wbs_hbm)
 
@@ -92,63 +95,90 @@ def tile_moe_adb_none_kernel(
         nc.tensor.transpose(turned[:, 0, :], gate_rows[:], ident[:])
         nc.scalar.activation(gate_cols[:], turned[:, 0, 0:S // P], COPY)
 
-        wb_cols = (E * PASSES - 1) * H
-        later = sb("later", [P, wb_cols + E * K + PASSES * K], U32, "slot_words")
-        wb_next = later[:, 0:wb_cols].rearrange("p (a i) -> p a i", i=H)
-        wa_w = later[:, wb_cols:wb_cols + E * K].rearrange("p (e k) -> p e k", k=K)
-        wt_w = later[:, wb_cols + E * K:].rearrange("p (s k) -> p s k", k=K)
-        for e in range(E):
-            a0 = max(e * PASSES, 1)
-            nc.sync.dma_start(out=wb_next[:, a0 - 1:(e + 1) * PASSES - 1, :].bitcast(I32), in_=wb_all[:, a0:(e + 1) * PASSES, :])
-        nc.sync.dma_start(out=wa_w.bitcast(I32), in_=wa_hbm)
-        nc.sync.dma_start(out=wt_w.bitcast(I32), in_=wt_hbm)
-        wb_w = [wb_first[:]] + [wb_next[:, a, :] for a in range(E * PASSES - 1)]
+        def carve(name, widths):
+            tile = sb(name + "_sb", [P, sum(widths)], U32, name)
+            ends = [sum(widths[:n + 1]) for n in range(len(widths))]
+            return [tile[:, end - width:end] for width, end in zip(widths, ends)]
 
-        g_s = {}
+        def load_words(dst, hbm):
+            view = dst.rearrange("p (a c) -> p a c", a=hbm.shape[1])
+            nc.sync.dma_start(out=view.bitcast(I32), in_=hbm)
+            return [view[:, a, :] for a in range(hbm.shape[1])]
 
-        def gather_bytes(j0, size):
-            scales = sb("g_s%d" % j0, [P, size], U8, {0: "slot_was", P: "slot_wts"}.get(j0))
-            nc.vector.tensor_copy(scales[:], dy_s[:].indirect(offs_sb[:, j0 // 16:(j0 + size) // 16]))
-            for j in range(j0, j0 + size, P):
-                g_s[j] = (scales, j - j0)
+        def load_planes(dst, row0, hbm):
+            nc.gpsimd.memset(dst.bitcast(I32), 0)
+            planes = dst.bitcast(U8).rearrange("p (a c) -> p a c", a=hbm.shape[1])
+            load_scales(nc.sync, planes, row0, hbm)
+            return planes
 
-        def gather_words(j):
-            words = []
-            for s in range(PASSES):
-                tile = keep.tile([P, P], U32, name="g_w%d" % s, tag="g_w%d" % s, bufs=AHEAD, align_bytes=64)
-                nc.vector.tensor_copy(tile[:], dy_w[s].indirect(offs_sb[:, j // 16:(j + P) // 16]))
-                words.append(tile)
-            return words
+        runs = [(0, 1), (1, PASSES)] + [(e * PASSES, (e + 1) * PASSES) for e in range(1, E)]
+        parts = carve("slot_words", [(a1 - a0) * H for a0, a1 in runs] + [E * K, E * K // 4])
+        wb_w = []
+        for part, (a0, a1) in zip(parts, runs):
+            wb_w.extend(load_words(part, wb_all[:, a0:a1, :]))
+        wa_w = load_words(parts[-2], wa_hbm)
+        wa_s = load_planes(parts[-1], WA_ROW, was_hbm)
+
+        g_s, g_w, late = {}, {}, []
+
+        def gather(j0):
+            if j0 in BYTE_GATHERS:
+                size = BYTE_GATHERS[j0]
+                scales = sb("g_s%d" % j0, [P, size], U8)
+                nc.vector.tensor_copy(scales[:], dy_s[:].indirect(offs_sb[:, j0 // 16:(j0 + size) // 16]))
+                for j in range(j0, j0 + size, P):
+                    g_s[j] = scales[:, j - j0:j - j0 + P]
+            if j0 in WORD_GATHERS:
+                size = WORD_GATHERS[j0]
+                for s in range(PASSES):
+                    if (j0, s) in EARLY_WORDS:
+                        tile = sb("g_w%d_%d" % (j0, s), [P, size], U32, EARLY_WORDS[(j0, s)])[:]
+                    else:
+                        if not late:
+                            late.append(sb("late_sb", [P, PASSES, S - C], U32, "late_words"))
+                        tile = late[0][:, s, j0 - C:j0 - C + size]
+                    nc.vector.tensor_copy(tile, dy_w[s].indirect(offs_sb[:, j0 // 16:(j0 + size) // 16]))
+                    for j in range(j0, j0 + size, P):
+                        g_w[(j, s)] = tile[:, j - j0:j - j0 + P]
+
+        def bank(n, shape):
+            return psum.tile(shape, F32, name="bank%d" % n, tag="bank%d" % n)
 
         def stage1(j):
             e = j // C
-            if j in dict(BYTE_GATHERS):
-                gather_bytes(j, dict(BYTE_GATHERS)[j])
-            words = gather_words(j)
-            scales, c0 = g_s[j]
-            acc = psum.tile([P, H], F32, name="acc1", tag="acc", bufs=5)
-            for s in range(PASSES):
-                nc.tensor.matmul_mx(
-                    out=acc[:],
-                    lhsT=words[s][:].bitcast(X4),
-                    lhsT_scale=scales[4 * s:P, c0:c0 + P],
-                    rhs=wb_w[e * PASSES + s].bitcast(X4),
-                    rhs_scale=wb_s[WB_ROW:P, e * PASSES + s, :],
-                    start=(s == 0), stop=(s == PASSES - 1),
-                )
-            dh = sb("dh%d" % (j // P), [P, 2, P, 2], BF16)
-            nc.scalar.activation(dh[:], acc[:].rearrange("j (p u v) -> j u p v", u=2, v=2), COPY,
-                                 scale=gate_cols[:, j // P:j // P + 1])
+            gather(j)
+            m = j // P
+            dh = sb("dh%d" % m, [P, 2, P, 2], BF16)
+            banks = (3, 1) if j == S - P else (m % 4,)
+            width = H // len(banks)
+            for n, b in enumerate(banks):
+                acc = bank(b, [P, width])
+                cols = slice(n * width, (n + 1) * width)
+                for s in range(PASSES):
+                    nc.tensor.matmul_mx(
+                        out=acc[:],
+                        lhsT=g_w[(j, s)].bitcast(X4),
+                        lhsT_scale=g_s[j][4 * s:P, :],
+                        rhs=wb_w[e * PASSES + s][:, cols].bitcast(X4),
+                        rhs_scale=wb_s[WB_ROW:P, e * PASSES + s, cols],
+                        start=(s == 0), stop=(s == PASSES - 1),
+                    )
+                dst = dh[:, :, n * width // 4:(n + 1) * width // 4, :]
+                src = acc[:].rearrange("j (p u v) -> j u p v", u=2, v=2)
+                if n == 0:
+                    nc.scalar.activation(dst, src, COPY, scale=gate_cols[:, m:m + 1])
+                else:
+                    nc.vector.tensor_scalar(dst, src, gate_cols[:, m:m + 1], None, MULT)
             return dh
 
         def turn(n, j0, size, dhs):
-            bank = psum.tile([P, 4, P], F32, name="turned", tag="turned", bufs=2)
+            turned = psum.tile([P, 4, P], F32, name="turned", tag="turned", bufs=2)
             for m, dh in enumerate(dhs):
                 pairs = dh[:].rearrange("j u p v -> j (u p v)").bitcast(F32)
                 for u in range(2):
-                    nc.tensor.transpose(bank[:, 2 * m + u, :], pairs[:, u * P:(u + 1) * P], ident[:])
+                    nc.tensor.transpose(turned[:, 2 * m + u, :], pairs[:, u * P:(u + 1) * P], ident[:])
             dht = sb("dht%d" % n, [P, size // P, P, 2], F32)
-            nc.scalar.copy(dht[:], bank[:, 0:2 * len(dhs), :].rearrange("p (m u) j -> p m j u", u=2))
+            nc.scalar.copy(dht[:], turned[:, 0:2 * len(dhs), :].rearrange("p (m u) j -> p m j u", u=2))
             return dht
 
         dhts = []
@@ -156,12 +186,9 @@ def tile_moe_adb_none_kernel(
             dhs = [stage1(j) for j in range(j0, j0 + size, P)]
             dhts.append(turn(n, j0, size, dhs))
             if n == 0:
-                wa_s = sb("wa_s", [P, E, K], U8, "slot_was")
-                nc.gpsimd.memset(wa_s[:].bitcast(I32), 0)
-                load_scales(nc.sync, wa_s, WA_ROW, was_hbm)
-                wt_s = sb("wt_s", [P, PASSES, K], U8, "slot_wts")
-                nc.gpsimd.memset(wt_s[:].bitcast(I32), 0)
-                load_scales(nc.sync, wt_s, WT_ROW, wts_hbm)
+                words_t, planes_t = carve("frozen_loads", [PASSES * K, PASSES * K // 4])
+                wt_w = load_words(words_t, wt_hbm)
+                wt_s = load_planes(planes_t, WT_ROW, wts_hbm)
 
         dx = sb("dx", [P, 2, S], F32)
         for n, (j0, size) in enumerate(UNITS):
@@ -170,51 +197,64 @@ def tile_moe_adb_none_kernel(
             plane = sb("dh_s%d" % n, [P, size], U8)
             nc.vector.quantize_mx(out=codes[:].bitcast(X4), scales=plane[:],
                                   in_=dhts[n][:].rearrange("p m j u -> p (m j u)").bitcast(BF16))
-            acc = psum.tile([P, 2, C], F32, name="acc2", tag="acc", bufs=5)
+            last = n == len(UNITS) - 1
+            if last:
+                accs = [bank(5 - h, [P, size])[:] for h in range(2)]
+            else:
+                acc = bank(DX_BANKS[n], [P, 2, size])
+                accs = [acc[:, h, :] for h in range(2)]
             for h in range(2):
                 nc.tensor.matmul_mx(
-                    out=acc[:, h, 0:size],
-                    lhsT=wa_w[:, e, h * P:(h + 1) * P].bitcast(X4),
+                    out=accs[h],
+                    lhsT=wa_w[e][:, h * P:(h + 1) * P].bitcast(X4),
                     lhsT_scale=wa_s[WA_ROW:P, e, h * P:(h + 1) * P],
                     rhs=codes[:].bitcast(X4), rhs_scale=plane[:],
                     start=True, stop=True,
                 )
-            if n in DX_ON_VECTOR:
-                nc.vector.tensor_copy(dx[:, :, j0:j0 + size], acc[:, :, 0:size])
+            if last:
+                for h in range(2):
+                    nc.scalar.copy(dx[:, h, j0:j0 + size], accs[h])
+            elif n in DX_ON_VECTOR:
+                nc.vector.tensor_copy(dx[:, :, j0:j0 + size], acc[:])
             else:
-                nc.scalar.copy(dx[:, :, j0:j0 + size], acc[:, :, 0:size])
+                nc.scalar.copy(dx[:, :, j0:j0 + size], acc[:])
 
         base = []
         for h in range(2):
-            acc = psum.tile([P, T], F32, name="base%d" % h, tag="acc", bufs=5)
+            acc = bank((2, 4)[h], [P, T])
             for s in range(PASSES):
                 nc.tensor.matmul_mx(
                     out=acc[:],
-                    lhsT=wt_w[:, s, h * P:(h + 1) * P].bitcast(X4),
+                    lhsT=wt_w[s][:, h * P:(h + 1) * P].bitcast(X4),
                     lhsT_scale=wt_s[WT_ROW:P, s, h * P:(h + 1) * P],
                     rhs=dy_w[s].bitcast(X4), rhs_scale=dy_s[4 * s:P, :],
                     start=(s == 0), stop=(s == PASSES - 1),
                 )
-            base.append(acc)
+            base.append(sb("base_sb%d" % h, [P, T], F32))
+            nc.scalar.copy(base[h][:], acc[:])
 
-        pending = None
-        for h in range(2):
-            for t0 in range(0, T, PIECE):
-                cols = slice(t0 // 16, (t0 + PIECE) // 16)
-                tag = "%d_%d" % (h, t0)
-                first = sb("first" + tag, [P, PIECE], F32)
-                second = sb("second" + tag, [P, PIECE], F32)
-                part = sb("part" + tag, [P, PIECE], F32)
-                total = sb("total" + tag, [P, PIECE], F32)
-                nc.vector.tensor_copy(first[:], dx[:, h, :].indirect(pos_sb[0][:, cols]))
-                if pending is not None:
-                    pending()
-                nc.vector.tensor_copy(second[:], dx[:, h, :].indirect(pos_sb[1][:, cols]))
-                nc.vector.tensor_tensor(part[:], base[h][:, t0:t0 + PIECE], first[:], ADD)
-
-                def finish(h=h, t0=t0, part=part, second=second, total=total):
-                    nc.vector.tensor_tensor(total[:], part[:], second[:], ADD)
-                    nc.sync.dma_start(out=out[h * P:(h + 1) * P, t0:t0 + PIECE], in_=total[:])
-
-                pending = finish
-        pending()
+        for n, (h, t0, size) in enumerate(PIECES):
+            cols = slice(t0 // 16, (t0 + size) // 16)
+            first = sb("first%d" % n, [P, size], F32)
+            second = sb("second%d" % n, [P, size], F32)
+            total = sb("total%d" % n, [P, size], F32)
+            nc.vector.tensor_copy(first[:], dx[:, h, :].indirect(pos_sb[0][:, cols]))
+            nc.vector.tensor_copy(second[:], dx[:, h, :].indirect(pos_sb[1][:, cols]))
+            if n >= ON_TENSOR:
+                part = sb("part%d" % n, [P, size], F32)
+                nc.vector.tensor_tensor(part[:], base[h][:, t0:t0 + size], first[:], ADD)
+                nc.vector.tensor_tensor(total[:], part[:], second[:], ADD)
+            else:
+                blocks = size // P
+                summed = bank((0, 1, 3)[n], [P, blocks, P])
+                for m in range(blocks):
+                    terms = (base[h][:, t0 + m * P:t0 + (m + 1) * P], first[:, m * P:(m + 1) * P], second[:, m * P:(m + 1) * P])
+                    for a, term in enumerate(terms):
+                        nc.tensor.matmul(summed[:, m, :], term, ident[:], start=(a == 0), stop=(a == 2), is_transpose=True)
+                sum_sb = sb("sum%d" % n, [P, blocks, P], F32)
+                nc.scalar.copy(sum_sb[:], summed[:])
+                back = psum.tile([P, 4, P], F32, name="turned", tag="turned", bufs=2)
+                for m in range(blocks):
+                    nc.tensor.transpose(back[:, m, :], sum_sb[:, m, :], ident[:])
+                nc.scalar.copy(total[:].rearrange("k (m t) -> k m t", t=P), back[:, 0:blocks, :])
+            nc.sync.dma_start(out=out[h * P:(h + 1) * P, t0:t0 + size], in_=total[:])

@@ -20,15 +20,11 @@ COPY = mybir.ActivationFunctionType.Copy
 ADD = mybir.AluOpType.add
 MULT = mybir.AluOpType.mult
 
-BYTE_GATHERS = {0: 128, 128: 128, 256: 256, 512: 256, 768: 256}
-WORD_GATHERS = {0: 128, 128: 128, 256: 256, 512: 256, 768: 128, 896: 128}
-EARLY_WORDS = {(0, 0): "late_words", (0, 1): None, (0, 2): None,
-               (128, 0): "frozen_loads", (128, 1): None, (128, 2): None, (256, 0): None}
-DX_ON_VECTOR = (0, 1, 2)
-DX_BANKS = (4, 5, 4, 3)
-PIECES = [(0, 0, 256), (0, 256, 256), (1, 0, 128), (1, 128, 256), (1, 384, 128)]
-ON_TENSOR = 3
+QUADRANTS = (0, 2, 1, 3)
+WB_FIRST_ROW, WB_REST_ROW, WT_ROW, WA_ROW = 0, 4, 8, 12
 UNITS = [(0, 256), (256, 256), (512, 256), (768, 128), (896, 128)]
+TURN_BANKS = (2, 4, 0, 2, 7)
+DX_BANKS = ((3, 5), (4, 6), (3, 5), (4, 6), (0, 2))
 
 
 def tile_moe_adb_none_kernel(
@@ -38,6 +34,7 @@ def tile_moe_adb_none_kernel(
     nc = tc.nc
     with ExitStack() as ctx:
         keep = ctx.enter_context(tc.tile_pool(name="keep", bufs=1))
+        ring = ctx.enter_context(tc.tile_pool(name="ring", bufs=1))
         psum = ctx.enter_context(tc.psum_pool(name="psum", bufs=1))
 
         def sb(name, shape, dtype, slot=None):
@@ -47,18 +44,27 @@ def tile_moe_adb_none_kernel(
         pos_sb = [keep.tile([P, T // 16], U16, name="pos%d_sb" % r) for r in range(2)]
 
         dy_first = sb("dy_first", [P, T], U32)
-        dy_rest = sb("dy_rest", [P, PASSES - 1, T], U32)
-        dy_w = [dy_first[:]] + [dy_rest[:, s, :] for s in range(PASSES - 1)]
         dy_s = sb("dy_s", [P, T], U8)
-        wb_s = sb("wb_s", [P, E * PASSES, H], U8)
-        gate_rows = sb("gate_rows", [P, P], F32, "slot_words")
+        wb_s_first = sb("wb_s_first", [P, PASSES, H], U8)
+        wb_s_rest = sb("wb_s_rest", [P, (E - 1) * PASSES, H], U8)
+        wa_s = sb("wa_s", [P, E, K], U8)
+        wt_s = sb("wt_s", [P, PASSES, K], U8)
+        gate_rows = sb("gate_rows", [P, P], F32)
         gate_cols = sb("gate_cols", [P, S // P], F32)
         ident = sb("ident", [P, P], F32)
 
         nc.gpsimd.memset(dy_s[:].bitcast(I32), 0)
-        nc.vector.memset(wb_s[:].bitcast(I32), 0)
+        nc.gpsimd.memset(gate_rows[:], 0.0)
+        make_identity(nc, ident[:])
+        nc.vector.memset(wb_s_first[:].bitcast(I32), 0)
+        nc.vector.memset(wb_s_rest[:].bitcast(I32), 0)
+        nc.vector.memset(wa_s[:].bitcast(I32), 0)
+        nc.vector.memset(wt_s[:].bitcast(I32), 0)
+        dy_rest = sb("dy_rest", [P, PASSES - 1, T], U32)
+        dy_w = [dy_first[:]] + [dy_rest[:, s, :] for s in range(PASSES - 1)]
 
         dy_hbm = dy_words.rearrange("s p t d -> p s (t d)").bitcast(I32)
+        wb_hbm = wbt_words.rearrange("e s p i d -> p (e s) (i d)").bitcast(I32)
         wa_hbm = wat_words.rearrange("e s p k d -> p (e s) (k d)").bitcast(I32)
         wt_hbm = wt_words.rearrange("s p k d -> p s (k d)").bitcast(I32)
         dys_hbm = dy_scales.bitcast(I32)
@@ -70,33 +76,19 @@ def tile_moe_adb_none_kernel(
             queue.dma_start(out=dy_s[32 * q:32 * q + 4 * PASSES, :].bitcast(I32), in_=dys_hbm[:, 4 * q:4 * q + 4, :])
 
         def load_scales(queue, tile, row0, hbm):
-            for q in range(4):
+            for q in QUADRANTS:
                 queue.dma_start(out=tile[32 * q + row0:32 * q + row0 + 4, :, :].bitcast(I32), in_=hbm[4 * q:4 * q + 4])
 
-        WB_ROW = 0
-        WT_ROW = 8
-        WA_ROW = 12
-
         nc.sync.dma_start(offs_sb[:], offs)
-        nc.scalar.dma_start(out=gate_rows[:], in_=gate.rearrange("r (c p) -> (r c) p", p=P)[0:P, :])
-        nc.sync.dma_start(pos_sb[0][:], pos1)
-        nc.sync.dma_start(pos_sb[1][:], pos2)
         nc.sync.dma_start(out=dy_first[:].bitcast(I32), in_=dy_hbm[:, 0, :])
         nc.sync.dma_start(out=dy_rest[:].bitcast(I32), in_=dy_hbm[:, 1:PASSES, :])
-        wb_all = wbt_words.rearrange("e s p i d -> p (e s) (i d)").bitcast(I32)
-        make_identity(nc, ident[:])
         load_dy_scales(nc.scalar, 0)
+        load_dy_scales(nc.sync, 2)
         load_dy_scales(nc.scalar, 1)
-        load_dy_scales(nc.scalar, 2)
         load_dy_scales(nc.sync, 3)
-        load_scales(nc.sync, wb_s, WB_ROW, wbs_hbm)
-
-        turned = psum.tile([P, 4, P], F32, name="turned", tag="turned", bufs=2)
-        nc.tensor.transpose(turned[:, 0, :], gate_rows[:], ident[:])
-        nc.scalar.activation(gate_cols[:], turned[:, 0, 0:S // P], COPY)
 
         def carve(name, widths):
-            tile = sb(name + "_sb", [P, sum(widths)], U32, name)
+            tile = sb(name, [P, sum(widths)], U32)
             ends = [sum(widths[:n + 1]) for n in range(len(widths))]
             return [tile[:, end - width:end] for width, end in zip(widths, ends)]
 
@@ -105,51 +97,60 @@ def tile_moe_adb_none_kernel(
             nc.sync.dma_start(out=view.bitcast(I32), in_=hbm)
             return [view[:, a, :] for a in range(hbm.shape[1])]
 
-        def load_planes(dst, row0, hbm):
-            nc.gpsimd.memset(dst.bitcast(I32), 0)
-            planes = dst.bitcast(U8).rearrange("p (a c) -> p a c", a=hbm.shape[1])
-            load_scales(nc.sync, planes, row0, hbm)
-            return planes
-
-        runs = [(0, 1), (1, PASSES)] + [(e * PASSES, (e + 1) * PASSES) for e in range(1, E)]
-        parts = carve("slot_words", [(a1 - a0) * H for a0, a1 in runs] + [E * K, E * K // 4])
+        runs = [(0, 3), (3, 6), (6, 9), (9, 11), (11, 12)]
+        parts = carve("late_loads", [(a1 - a0) * H for a0, a1 in runs] + [E * K, PASSES * K])
         wb_w = []
-        for part, (a0, a1) in zip(parts, runs):
-            wb_w.extend(load_words(part, wb_all[:, a0:a1, :]))
+        for n, (a0, a1) in enumerate(runs):
+            wb_w.extend(load_words(parts[n], wb_hbm[:, a0:a1, :]))
+            if n == 0:
+                nc.sync.dma_start(out=gate_rows[0:S // P, :], in_=gate.rearrange("r (c p) -> (r c) p", p=P)[0:S // P, :])
+                load_scales(nc.sync, wb_s_first, WB_FIRST_ROW, wbs_hbm[:, 0:PASSES, :])
+            if n == 1:
+                load_scales(nc.sync, wb_s_rest, WB_REST_ROW, wbs_hbm[:, PASSES:E * PASSES, :])
+        wb_s = ([wb_s_first[WB_FIRST_ROW:P, s, :] for s in range(PASSES)]
+                + [wb_s_rest[WB_REST_ROW:P, a, :] for a in range((E - 1) * PASSES)])
+        load_scales(nc.sync, wa_s, WA_ROW, was_hbm)
         wa_w = load_words(parts[-2], wa_hbm)
-        wa_s = load_planes(parts[-1], WA_ROW, was_hbm)
-
-        g_s, g_w, late = {}, {}, []
-
-        def gather(j0):
-            if j0 in BYTE_GATHERS:
-                size = BYTE_GATHERS[j0]
-                scales = sb("g_s%d" % j0, [P, size], U8)
-                nc.vector.tensor_copy(scales[:], dy_s[:].indirect(offs_sb[:, j0 // 16:(j0 + size) // 16]))
-                for j in range(j0, j0 + size, P):
-                    g_s[j] = scales[:, j - j0:j - j0 + P]
-            if j0 in WORD_GATHERS:
-                size = WORD_GATHERS[j0]
-                for s in range(PASSES):
-                    if (j0, s) in EARLY_WORDS:
-                        tile = sb("g_w%d_%d" % (j0, s), [P, size], U32, EARLY_WORDS[(j0, s)])[:]
-                    else:
-                        if not late:
-                            late.append(sb("late_sb", [P, PASSES, S - C], U32, "late_words"))
-                        tile = late[0][:, s, j0 - C:j0 - C + size]
-                    nc.vector.tensor_copy(tile, dy_w[s].indirect(offs_sb[:, j0 // 16:(j0 + size) // 16]))
-                    for j in range(j0, j0 + size, P):
-                        g_w[(j, s)] = tile[:, j - j0:j - j0 + P]
+        load_scales(nc.sync, wt_s, WT_ROW, wts_hbm)
+        wt_w = load_words(parts[-1], wt_hbm)
+        nc.sync.dma_start(pos_sb[0][:], pos1)
+        nc.sync.dma_start(pos_sb[1][:], pos2)
 
         def bank(n, shape):
             return psum.tile(shape, F32, name="bank%d" % n, tag="bank%d" % n)
 
+        gate_turned = bank(7, [P, P])
+        nc.tensor.transpose(gate_turned[:], gate_rows[:], ident[:])
+        nc.scalar.activation(gate_cols[:], gate_turned[:, 0:S // P], COPY)
+
+        late_bytes_width = S - C
+        first_words = ring.tile([P, P], U32, name="first_words", offset=late_bytes_width - 256, align_bytes=64)
+        g_s, g_w = {}, {}
+
+        def gather_bytes(tile, j0):
+            size = tile.shape[1]
+            nc.vector.tensor_copy(tile, dy_s[:].indirect(offs_sb[:, j0 // 16:(j0 + size) // 16]))
+            for j in range(j0, j0 + size, P):
+                g_s[j] = tile[:, j - j0:j - j0 + P]
+
+        def gather_words(tile, j0, s):
+            size = tile.shape[1]
+            nc.vector.tensor_copy(tile, dy_w[s].indirect(offs_sb[:, j0 // 16:(j0 + size) // 16]))
+            for j in range(j0, j0 + size, P):
+                g_w[(j, s)] = tile[:, j - j0:j - j0 + P]
+
+        gather_words(first_words[:], 0, 0)
+        gather_words(sb("early0", [P, 256], U32)[:], 128, 0)
+        gather_words(sb("early1", [P, 384], U32)[:], 384, 0)
+        gather_bytes(sb("early_s", [P, C], U8)[:], 0)
+        gather_words(sb("early2", [P, C], U32)[:], 0, 1)
+        gather_words(sb("early3", [P, C], U32)[:], 0, 2)
+
         def stage1(j):
             e = j // C
-            gather(j)
             m = j // P
             dh = sb("dh%d" % m, [P, 2, P, 2], BF16)
-            banks = (3, 1) if j == S - P else (m % 4,)
+            banks = (7, 1) if j == S - P else (m,)
             width = H // len(banks)
             for n, b in enumerate(banks):
                 acc = bank(b, [P, width])
@@ -160,7 +161,7 @@ def tile_moe_adb_none_kernel(
                         lhsT=g_w[(j, s)].bitcast(X4),
                         lhsT_scale=g_s[j][4 * s:P, :],
                         rhs=wb_w[e * PASSES + s][:, cols].bitcast(X4),
-                        rhs_scale=wb_s[WB_ROW:P, e * PASSES + s, cols],
+                        rhs_scale=wb_s[e * PASSES + s][:, cols],
                         start=(s == 0), stop=(s == PASSES - 1),
                     )
                 dst = dh[:, :, n * width // 4:(n + 1) * width // 4, :]
@@ -171,57 +172,40 @@ def tile_moe_adb_none_kernel(
                     nc.vector.tensor_scalar(dst, src, gate_cols[:, m:m + 1], None, MULT)
             return dh
 
-        def turn(n, j0, size, dhs):
-            turned = psum.tile([P, 4, P], F32, name="turned", tag="turned", bufs=2)
+        def turn(n, dhs):
+            turned = bank(TURN_BANKS[n], [P, 4, P])
             for m, dh in enumerate(dhs):
                 pairs = dh[:].rearrange("j u p v -> j (u p v)").bitcast(F32)
                 for u in range(2):
                     nc.tensor.transpose(turned[:, 2 * m + u, :], pairs[:, u * P:(u + 1) * P], ident[:])
-            dht = sb("dht%d" % n, [P, size // P, P, 2], F32)
+            dht = sb("dht%d" % n, [P, len(dhs), P, 2], F32)
             nc.scalar.copy(dht[:], turned[:, 0:2 * len(dhs), :].rearrange("p (m u) j -> p m j u", u=2))
             return dht
 
+        dhs = [stage1(0), stage1(P)]
+        late_bytes = ring.tile([P, late_bytes_width], U8, name="late_bytes", offset=0, align_bytes=64)
+        late_words = ring.tile([P, 2 * (S - C) + C], U32, name="late_words", offset=late_bytes_width, align_bytes=64)
+        gather_bytes(late_bytes[:, 0:384], C)
+        gather_words(late_words[:, 0:C], C, 1)
+        gather_words(late_words[:, C:2 * C], C, 2)
+        gather_bytes(late_bytes[:, 384:768], C + 384)
+        gather_words(late_words[:, 2 * C:3 * C], 2 * C, 1)
+        gather_words(late_words[:, 3 * C:4 * C], 2 * C, 2)
+        gather_words(late_words[:, 4 * C:5 * C], 3 * C, 0)
+        gather_words(late_words[:, 5 * C:6 * C], 3 * C, 1)
+        gather_words(late_words[:, 6 * C:6 * C + P], 3 * C, 2)
+        gather_words(late_words[:, 6 * C + P:7 * C], 3 * C + P, 2)
+
         dhts = []
         for n, (j0, size) in enumerate(UNITS):
-            dhs = [stage1(j) for j in range(j0, j0 + size, P)]
-            dhts.append(turn(n, j0, size, dhs))
-            if n == 0:
-                words_t, planes_t = carve("frozen_loads", [PASSES * K, PASSES * K // 4])
-                wt_w = load_words(words_t, wt_hbm)
-                wt_s = load_planes(planes_t, WT_ROW, wts_hbm)
+            if n + 1 < len(UNITS):
+                j1, size1 = UNITS[n + 1]
+                ahead = [stage1(j) for j in range(j1, j1 + size1, P)]
+            dhts.append(turn(n, dhs))
+            dhs = ahead
 
-        dx = sb("dx", [P, 2, S], F32)
-        for n, (j0, size) in enumerate(UNITS):
-            e = j0 // C
-            codes = sb("dh_w%d" % n, [P, size], U32)
-            plane = sb("dh_s%d" % n, [P, size], U8)
-            nc.vector.quantize_mx(out=codes[:].bitcast(X4), scales=plane[:],
-                                  in_=dhts[n][:].rearrange("p m j u -> p (m j u)").bitcast(BF16))
-            last = n == len(UNITS) - 1
-            if last:
-                accs = [bank(5 - h, [P, size])[:] for h in range(2)]
-            else:
-                acc = bank(DX_BANKS[n], [P, 2, size])
-                accs = [acc[:, h, :] for h in range(2)]
-            for h in range(2):
-                nc.tensor.matmul_mx(
-                    out=accs[h],
-                    lhsT=wa_w[e][:, h * P:(h + 1) * P].bitcast(X4),
-                    lhsT_scale=wa_s[WA_ROW:P, e, h * P:(h + 1) * P],
-                    rhs=codes[:].bitcast(X4), rhs_scale=plane[:],
-                    start=True, stop=True,
-                )
-            if last:
-                for h in range(2):
-                    nc.scalar.copy(dx[:, h, j0:j0 + size], accs[h])
-            elif n in DX_ON_VECTOR:
-                nc.vector.tensor_copy(dx[:, :, j0:j0 + size], acc[:])
-            else:
-                nc.scalar.copy(dx[:, :, j0:j0 + size], acc[:])
-
-        base = []
-        for h in range(2):
-            acc = bank((2, 4)[h], [P, T])
+        def frozen(h, b):
+            acc = bank(b, [P, T])
             for s in range(PASSES):
                 nc.tensor.matmul_mx(
                     out=acc[:],
@@ -230,31 +214,40 @@ def tile_moe_adb_none_kernel(
                     rhs=dy_w[s].bitcast(X4), rhs_scale=dy_s[4 * s:P, :],
                     start=(s == 0), stop=(s == PASSES - 1),
                 )
-            base.append(sb("base_sb%d" % h, [P, T], F32))
-            nc.scalar.copy(base[h][:], acc[:])
+            base = sb("base_sb%d" % h, [P, T], F32)
+            nc.scalar.copy(base[:], acc[:])
+            return base
 
-        for n, (h, t0, size) in enumerate(PIECES):
-            cols = slice(t0 // 16, (t0 + size) // 16)
-            first = sb("first%d" % n, [P, size], F32)
-            second = sb("second%d" % n, [P, size], F32)
-            total = sb("total%d" % n, [P, size], F32)
-            nc.vector.tensor_copy(first[:], dx[:, h, :].indirect(pos_sb[0][:, cols]))
-            nc.vector.tensor_copy(second[:], dx[:, h, :].indirect(pos_sb[1][:, cols]))
-            if n >= ON_TENSOR:
-                part = sb("part%d" % n, [P, size], F32)
-                nc.vector.tensor_tensor(part[:], base[h][:, t0:t0 + size], first[:], ADD)
-                nc.vector.tensor_tensor(total[:], part[:], second[:], ADD)
-            else:
-                blocks = size // P
-                summed = bank((0, 1, 3)[n], [P, blocks, P])
-                for m in range(blocks):
-                    terms = (base[h][:, t0 + m * P:t0 + (m + 1) * P], first[:, m * P:(m + 1) * P], second[:, m * P:(m + 1) * P])
-                    for a, term in enumerate(terms):
-                        nc.tensor.matmul(summed[:, m, :], term, ident[:], start=(a == 0), stop=(a == 2), is_transpose=True)
-                sum_sb = sb("sum%d" % n, [P, blocks, P], F32)
-                nc.scalar.copy(sum_sb[:], summed[:])
-                back = psum.tile([P, 4, P], F32, name="turned", tag="turned", bufs=2)
-                for m in range(blocks):
-                    nc.tensor.transpose(back[:, m, :], sum_sb[:, m, :], ident[:])
-                nc.scalar.copy(total[:].rearrange("k (m t) -> k m t", t=P), back[:, 0:blocks, :])
-            nc.sync.dma_start(out=out[h * P:(h + 1) * P, t0:t0 + size], in_=total[:])
+        dx = [sb("dx%d" % h, [P, S], F32) for h in range(2)]
+        for n, (j0, size) in enumerate(UNITS):
+            e = j0 // C
+            codes = sb("dh_w%d" % n, [P, size], U32)
+            plane = sb("dh_s%d" % n, [P, size], U8)
+            nc.vector.quantize_mx(out=codes[:].bitcast(X4), scales=plane[:],
+                                  in_=dhts[n][:].rearrange("p m j u -> p (m j u)").bitcast(BF16))
+            for h in range(2):
+                acc = bank(DX_BANKS[n][h], [P, size])
+                nc.tensor.matmul_mx(
+                    out=acc[:],
+                    lhsT=wa_w[e][:, h * P:(h + 1) * P].bitcast(X4),
+                    lhsT_scale=wa_s[WA_ROW:P, e, h * P:(h + 1) * P],
+                    rhs=codes[:].bitcast(X4), rhs_scale=plane[:],
+                    start=True, stop=True,
+                )
+                if h == 0:
+                    nc.vector.tensor_copy(dx[h][:, j0:j0 + size], acc[:])
+                else:
+                    nc.scalar.copy(dx[h][:, j0:j0 + size], acc[:])
+
+        base = [frozen(0, 1), frozen(1, DX_BANKS[-1][0])]
+
+        for h in range(2):
+            part = [sb("part%d_%d" % (h, n), [P, C], F32) for n in range(2)]
+            total = [sb("total%d_%d" % (h, n), [P, C], F32) for n in range(2)]
+            for n in range(2):
+                cols = slice(n * C // 16, (n + 1) * C // 16)
+                nc.vector.tensor_tensor(part[n][:], dx[h][:].indirect(pos_sb[0][:, cols]), base[h][:, n * C:(n + 1) * C], ADD)
+            for n in range(2):
+                cols = slice(n * C // 16, (n + 1) * C // 16)
+                nc.vector.tensor_tensor(total[n][:], dx[h][:].indirect(pos_sb[1][:, cols]), part[n][:], ADD)
+                nc.sync.dma_start(out=out[h * P:(h + 1) * P, n * C:(n + 1) * C], in_=total[n][:])

@@ -23,8 +23,11 @@ MULT = mybir.AluOpType.mult
 QUADRANTS = (0, 2, 1, 3)
 WB_FIRST_ROW, WB_REST_ROW, WT_ROW, WA_ROW = 0, 4, 8, 12
 UNITS = [(0, 256), (256, 256), (512, 256), (768, 128), (896, 128)]
-TURN_BANKS = (2, 4, 0, 2, 7)
-DX_BANKS = ((3, 5), (4, 6), (3, 5), (4, 6), (0, 2))
+LATE_GATHERS = [(384, 256, 0), (256, 256, 1), (256, 256, 2), (640, 384, None), (640, 384, 0), (512, 256, 1), (512, 256, 2),
+                (768, 256, 1), (768, 128, 2), (896, 128, 2)]
+TURNED_SUMS = [(0, 0), (0, 256)]
+SUM_BANKS = ((5, 2, 3), (7, 1, 4))
+TURN_BANKS = (2, 4, 6, 0, 1)
 
 
 def tile_moe_adb_none_kernel(
@@ -123,7 +126,7 @@ def tile_moe_adb_none_kernel(
         nc.tensor.transpose(gate_turned[:], gate_rows[:], ident[:])
         nc.scalar.activation(gate_cols[:], gate_turned[:, 0:S // P], COPY)
 
-        late_bytes_width = S - C
+        late_bytes_width = 384
         first_words = ring.tile([P, P], U32, name="first_words", offset=late_bytes_width - 256, align_bytes=64)
         g_s, g_w = {}, {}
 
@@ -141,10 +144,10 @@ def tile_moe_adb_none_kernel(
 
         gather_words(first_words[:], 0, 0)
         gather_words(sb("early0", [P, 256], U32)[:], 128, 0)
-        gather_words(sb("early1", [P, 384], U32)[:], 384, 0)
-        gather_bytes(sb("early_s", [P, C], U8)[:], 0)
+        gather_bytes(sb("early_s0", [P, C], U8)[:], 0)
         gather_words(sb("early2", [P, C], U32)[:], 0, 1)
         gather_words(sb("early3", [P, C], U32)[:], 0, 2)
+        gather_bytes(sb("early_s1", [P, 384], U8)[:], C)
 
         def stage1(j):
             e = j // C
@@ -152,10 +155,10 @@ def tile_moe_adb_none_kernel(
             dh = sb("dh%d" % m, [P, 2, P, 2], BF16)
             banks = (7, 1) if j == S - P else (m,)
             width = H // len(banks)
-            for n, b in enumerate(banks):
-                acc = bank(b, [P, width])
-                cols = slice(n * width, (n + 1) * width)
-                for s in range(PASSES):
+            accs = [bank(b, [P, width]) for b in banks]
+            for s in range(PASSES):
+                for n, acc in enumerate(accs):
+                    cols = slice(n * width, (n + 1) * width)
                     nc.tensor.matmul_mx(
                         out=acc[:],
                         lhsT=g_w[(j, s)].bitcast(X4),
@@ -164,6 +167,7 @@ def tile_moe_adb_none_kernel(
                         rhs_scale=wb_s[e * PASSES + s][:, cols],
                         start=(s == 0), stop=(s == PASSES - 1),
                     )
+            for n, acc in enumerate(accs):
                 dst = dh[:, :, n * width // 4:(n + 1) * width // 4, :]
                 src = acc[:].rearrange("j (p u v) -> j u p v", u=2, v=2)
                 if n == 0:
@@ -179,22 +183,20 @@ def tile_moe_adb_none_kernel(
                 for u in range(2):
                     nc.tensor.transpose(turned[:, 2 * m + u, :], pairs[:, u * P:(u + 1) * P], ident[:])
             dht = sb("dht%d" % n, [P, len(dhs), P, 2], F32)
-            nc.scalar.copy(dht[:], turned[:, 0:2 * len(dhs), :].rearrange("p (m u) j -> p m j u", u=2))
+            copy = nc.vector.tensor_copy if n == 2 else nc.scalar.copy
+            copy(dht[:], turned[:, 0:2 * len(dhs), :].rearrange("p (m u) j -> p m j u", u=2))
             return dht
 
         dhs = [stage1(0), stage1(P)]
         late_bytes = ring.tile([P, late_bytes_width], U8, name="late_bytes", offset=0, align_bytes=64)
-        late_words = ring.tile([P, 2 * (S - C) + C], U32, name="late_words", offset=late_bytes_width, align_bytes=64)
-        gather_bytes(late_bytes[:, 0:384], C)
-        gather_words(late_words[:, 0:C], C, 1)
-        gather_words(late_words[:, C:2 * C], C, 2)
-        gather_bytes(late_bytes[:, 384:768], C + 384)
-        gather_words(late_words[:, 2 * C:3 * C], 2 * C, 1)
-        gather_words(late_words[:, 3 * C:4 * C], 2 * C, 2)
-        gather_words(late_words[:, 4 * C:5 * C], 3 * C, 0)
-        gather_words(late_words[:, 5 * C:6 * C], 3 * C, 1)
-        gather_words(late_words[:, 6 * C:6 * C + P], 3 * C, 2)
-        gather_words(late_words[:, 6 * C + P:7 * C], 3 * C + P, 2)
+        late_words = ring.tile([P, 2 * (S - C) + 640], U32, name="late_words", offset=late_bytes_width, align_bytes=64)
+        at = 0
+        for j0, size, s in LATE_GATHERS:
+            if s is None:
+                gather_bytes(late_bytes[:], j0)
+            else:
+                gather_words(late_words[:, at:at + size], j0, s)
+                at += size
 
         dhts = []
         for n, (j0, size) in enumerate(UNITS):
@@ -219,35 +221,61 @@ def tile_moe_adb_none_kernel(
             return base
 
         dx = [sb("dx%d" % h, [P, S], F32) for h in range(2)]
+        codes, planes = [], []
         for n, (j0, size) in enumerate(UNITS):
-            e = j0 // C
-            codes = sb("dh_w%d" % n, [P, size], U32)
-            plane = sb("dh_s%d" % n, [P, size], U8)
-            nc.vector.quantize_mx(out=codes[:].bitcast(X4), scales=plane[:],
+            codes.append(sb("dh_w%d" % n, [P, size], U32))
+            planes.append(sb("dh_s%d" % n, [P, size], U8))
+            nc.vector.quantize_mx(out=codes[n][:].bitcast(X4), scales=planes[n][:],
                                   in_=dhts[n][:].rearrange("p m j u -> p (m j u)").bitcast(BF16))
-            for h in range(2):
-                acc = bank(DX_BANKS[n][h], [P, size])
+
+        def stage2(h, units, b, copy):
+            first = UNITS[units[0]][0]
+            width = sum(UNITS[n][1] for n in units)
+            acc = bank(b, [P, width])
+            for n in units:
+                j0, size = UNITS[n]
                 nc.tensor.matmul_mx(
-                    out=acc[:],
-                    lhsT=wa_w[e][:, h * P:(h + 1) * P].bitcast(X4),
-                    lhsT_scale=wa_s[WA_ROW:P, e, h * P:(h + 1) * P],
-                    rhs=codes[:].bitcast(X4), rhs_scale=plane[:],
+                    out=acc[:, j0 - first:j0 - first + size],
+                    lhsT=wa_w[j0 // C][:, h * P:(h + 1) * P].bitcast(X4),
+                    lhsT_scale=wa_s[WA_ROW:P, j0 // C, h * P:(h + 1) * P],
+                    rhs=codes[n][:].bitcast(X4), rhs_scale=planes[n][:],
                     start=True, stop=True,
                 )
-                if h == 0:
-                    nc.vector.tensor_copy(dx[h][:, j0:j0 + size], acc[:])
-                else:
-                    nc.scalar.copy(dx[h][:, j0:j0 + size], acc[:])
+            copy(dx[h][:, first:first + width], acc[:])
 
-        base = [frozen(0, 1), frozen(1, DX_BANKS[-1][0])]
+        stage2(0, (0, 1), 2, nc.scalar.copy)
+        stage2(0, (2,), 6, nc.scalar.copy)
+        stage2(0, (3,), 7, nc.vector.tensor_copy)
+        stage2(0, (4,), 1, nc.vector.tensor_copy)
+        base = [frozen(0, 0)]
+        stage2(1, (0, 1), 3, nc.scalar.copy)
+        stage2(1, (2, 3, 4), 4, nc.scalar.copy)
+        base.append(frozen(1, 6))
 
-        for h in range(2):
-            part = [sb("part%d_%d" % (h, n), [P, C], F32) for n in range(2)]
-            total = [sb("total%d_%d" % (h, n), [P, C], F32) for n in range(2)]
-            for n in range(2):
-                cols = slice(n * C // 16, (n + 1) * C // 16)
-                nc.vector.tensor_tensor(part[n][:], dx[h][:].indirect(pos_sb[0][:, cols]), base[h][:, n * C:(n + 1) * C], ADD)
-            for n in range(2):
-                cols = slice(n * C // 16, (n + 1) * C // 16)
-                nc.vector.tensor_tensor(total[n][:], dx[h][:].indirect(pos_sb[1][:, cols]), part[n][:], ADD)
-                nc.sync.dma_start(out=out[h * P:(h + 1) * P, n * C:(n + 1) * C], in_=total[n][:])
+        for n, (h, t0) in enumerate(TURNED_SUMS):
+            cols = slice(t0 // 16, (t0 + C) // 16)
+            picked = [sb("picked%d_%d" % (n, r), [P, C], F32) for r in range(2)]
+            for r in range(2):
+                nc.vector.tensor_copy(picked[r][:], dx[h][:].indirect(pos_sb[r][:, cols]))
+            summed = [bank(SUM_BANKS[n][m], [P, P]) for m in range(2)]
+            for a, term in enumerate((base[h][:, t0:t0 + C], picked[0][:], picked[1][:])):
+                for m in range(2):
+                    nc.tensor.matmul(summed[m][:], term[:, m * P:(m + 1) * P], ident[:], start=(a == 0), stop=(a == 2), is_transpose=True)
+            sum_sb = sb("sum%d" % n, [P, 2, P], F32)
+            back = bank(SUM_BANKS[n][2], [P, 2, P])
+            for m in range(2):
+                nc.scalar.copy(sum_sb[:, m, :], summed[m][:])
+                nc.tensor.transpose(back[:, m, :], sum_sb[:, m, :], ident[:])
+            total = sb("total%d" % n, [P, C], F32)
+            nc.scalar.copy(total[:].rearrange("k (m t) -> k m t", t=P), back[:])
+            nc.sync.dma_start(out=out[h * P:(h + 1) * P, t0:t0 + C], in_=total[:])
+
+        part = [sb("part%d" % n, [P, C], F32) for n in range(2)]
+        last = [sb("last%d" % n, [P, C], F32) for n in range(2)]
+        for n in range(2):
+            t0 = n * C
+            nc.vector.tensor_tensor(part[n][:], dx[1][:].indirect(pos_sb[0][:, t0 // 16:(t0 + C) // 16]), base[1][:, t0:t0 + C], ADD)
+        for n in range(2):
+            t0 = n * C
+            nc.vector.tensor_tensor(last[n][:], dx[1][:].indirect(pos_sb[1][:, t0 // 16:(t0 + C) // 16]), part[n][:], ADD)
+            nc.sync.dma_start(out=out[P:2 * P, t0:t0 + C], in_=last[n][:])

@@ -20,7 +20,6 @@ COPY = mybir.ActivationFunctionType.Copy
 ADD = mybir.AluOpType.add
 MULT = mybir.AluOpType.mult
 
-QUADRANTS = (0, 2, 1, 3)
 WB_FIRST_ROW, WB_REST_ROW, WT_ROW, WA_ROW = 0, 4, 8, 12
 UNITS = [(0, 256), (256, 256), (512, 256), (768, 128), (896, 128)]
 LATE_GATHERS = [(384, 256, 0), (256, 256, 1), (256, 256, 2), (640, 384, None), (640, 384, 0), (512, 256, 1), (512, 256, 2),
@@ -79,8 +78,8 @@ def tile_moe_adb_none_kernel(
             queue.dma_start(out=dy_s[32 * q:32 * q + 4 * PASSES, :].bitcast(I32), in_=dys_hbm[:, 4 * q:4 * q + 4, :])
 
         def load_scales(queue, tile, row0, hbm):
-            for q in QUADRANTS:
-                queue.dma_start(out=tile[32 * q + row0:32 * q + row0 + 4, :, :].bitcast(I32), in_=hbm[4 * q:4 * q + 4])
+            for r in range(4):
+                queue.dma_start(out=tile[row0 + r:P:32, :, :].bitcast(I32), in_=hbm[r:16:4])
 
         nc.sync.dma_start(offs_sb[:], offs)
         nc.sync.dma_start(out=dy_first[:].bitcast(I32), in_=dy_hbm[:, 0, :])

@@ -24,7 +24,8 @@ WB_FIRST_ROW, WB_REST_ROW, WT_ROW, WA_ROW = 0, 4, 8, 12
 UNITS = [(0, 256), (256, 256), (512, 256), (768, 128), (896, 128)]
 LATE_GATHERS = [(384, 256, 0), (256, 256, 1), (256, 256, 2), (640, 384, None), (640, 384, 0), (512, 256, 1), (512, 256, 2),
                 (768, 256, 1), (768, 128, 2), (896, 128, 2)]
-TURNED_SUMS = [(0, 0), (0, 256)]
+TURNED_SUMS = [(0, 0)]
+FUSED_SUMS = [(0, 256, 256), (1, 0, 512)]
 SUM_BANKS = ((5, 2, 3), (7, 1, 4))
 TURN_BANKS = (2, 4, 6, 0, 1)
 
@@ -267,14 +268,16 @@ def tile_moe_adb_none_kernel(
                 nc.tensor.transpose(back[:, m, :], sum_sb[:, m, :], ident[:])
             total = sb("total%d" % n, [P, C], F32)
             nc.scalar.copy(total[:].rearrange("k (m t) -> k m t", t=P), back[:])
-            nc.sync.dma_start(out=out[h * P:(h + 1) * P, t0:t0 + C], in_=total[:])
+            nc.scalar.dma_start(out=out[h * P:(h + 1) * P, t0:t0 + C], in_=total[:])
 
-        part = [sb("part%d" % n, [P, C], F32) for n in range(2)]
-        last = [sb("last%d" % n, [P, C], F32) for n in range(2)]
-        for n in range(2):
-            t0 = n * C
-            nc.vector.tensor_tensor(part[n][:], dx[1][:].indirect(pos_sb[0][:, t0 // 16:(t0 + C) // 16]), base[1][:, t0:t0 + C], ADD)
-        for n in range(2):
-            t0 = n * C
-            nc.vector.tensor_tensor(last[n][:], dx[1][:].indirect(pos_sb[1][:, t0 // 16:(t0 + C) // 16]), part[n][:], ADD)
-            nc.sync.dma_start(out=out[P:2 * P, t0:t0 + C], in_=last[n][:])
+        for h, t0, size in FUSED_SUMS:
+            half = size // 2
+            part = sb("part%d" % h, [P, size], F32)
+            last = [sb("last%d_%d" % (h, n), [P, half], F32) for n in range(2)]
+            cols = [slice((t0 + n * half) // 16, (t0 + (n + 1) * half) // 16) for n in range(2)]
+            for n in range(2):
+                nc.vector.tensor_tensor(part[:, n * half:(n + 1) * half], dx[h][:].indirect(pos_sb[0][:, cols[n]]),
+                                        base[h][:, t0 + n * half:t0 + (n + 1) * half], ADD)
+            for n in range(2):
+                nc.vector.tensor_tensor(last[n][:], dx[h][:].indirect(pos_sb[1][:, cols[n]]), part[:, n * half:(n + 1) * half], ADD)
+                nc.sync.dma_start(out=out[h * P:(h + 1) * P, t0 + n * half:t0 + (n + 1) * half], in_=last[n][:])

@@ -22,11 +22,12 @@ MULT = mybir.AluOpType.mult
 
 WB_FIRST_ROW, WB_REST_ROW, WT_ROW, WA_ROW = 0, 4, 8, 12
 UNITS = [(0, 256), (256, 256), (512, 256), (768, 128), (896, 128)]
-LATE_GATHERS = [(384, 256, 0), (256, 256, 1), (256, 256, 2), (640, 384, None), (640, 384, 0), (512, 256, 1), (512, 256, 2),
+LATE_GATHERS = [(128, 128, 1), (128, 128, 2), (384, 256, 0), (256, 256, 1), (256, 256, 2), (640, 384, 0), (512, 256, 1), (512, 256, 2),
                 (768, 256, 1), (768, 128, 2), (896, 128, 2)]
 TURNED_SUMS = [(0, 0)]
 FUSED_SUMS = [(0, 256, 256), (1, 0, 512)]
 SUM_BANKS = ((5, 2, 3), (7, 1, 4))
+WARM_PASSES = 2
 TURN_BANKS = (2, 4, 6, 0, 1)
 
 
@@ -37,7 +38,6 @@ def tile_moe_adb_none_kernel(
     nc = tc.nc
     with ExitStack() as ctx:
         keep = ctx.enter_context(tc.tile_pool(name="keep", bufs=1))
-        ring = ctx.enter_context(tc.tile_pool(name="ring", bufs=1))
         psum = ctx.enter_context(tc.psum_pool(name="psum", bufs=1))
 
         def sb(name, shape, dtype, slot=None):
@@ -126,8 +126,7 @@ def tile_moe_adb_none_kernel(
         nc.tensor.transpose(gate_turned[:], gate_rows[:], ident[:])
         nc.scalar.activation(gate_cols[:], gate_turned[:, 0:S // P], COPY)
 
-        late_bytes_width = 384
-        first_words = ring.tile([P, P], U32, name="first_words", offset=late_bytes_width - 256, align_bytes=64)
+        first_words = sb("first_words", [P, P], U32, "late_words")
         g_s, g_w = {}, {}
 
         def gather_bytes(tile, j0):
@@ -143,11 +142,19 @@ def tile_moe_adb_none_kernel(
                 g_w[(j, s)] = tile[:, j - j0:j - j0 + P]
 
         gather_words(first_words[:], 0, 0)
-        gather_words(sb("early0", [P, 256], U32)[:], 128, 0)
-        gather_bytes(sb("early_s0", [P, C], U8)[:], 0)
-        gather_words(sb("early2", [P, C], U32)[:], 0, 1)
-        gather_words(sb("early3", [P, C], U32)[:], 0, 2)
+        early_words = sb("early0", [P, 256], U32)
+        early_bytes = sb("early_s0", [P, C], U8)
+        gather_words(early_words[:], 128, 0)
+        gather_words(sb("early2", [P, P], U32)[:], 0, 1)
+        gather_words(sb("early3", [P, P], U32)[:], 0, 2)
+        gather_bytes(early_bytes[:], 0)
         gather_bytes(sb("early_s1", [P, 384], U8)[:], C)
+        gather_bytes(sb("early_s2", [P, 384], U8)[:], C + 384)
+
+        warm = bank(5, [P, C])
+        for n in range(WARM_PASSES):
+            nc.tensor.matmul_mx(out=warm[:], lhsT=early_words[:, 0:P].bitcast(X4), lhsT_scale=early_bytes[:, 0:P],
+                                rhs=early_words[:].bitcast(X4), rhs_scale=early_bytes[:], start=True, stop=True)
 
         def stage1(j):
             e = j // C
@@ -187,16 +194,13 @@ def tile_moe_adb_none_kernel(
             copy(dht[:], turned[:, 0:2 * len(dhs), :].rearrange("p (m u) j -> p m j u", u=2))
             return dht
 
-        dhs = [stage1(0), stage1(P)]
-        late_bytes = ring.tile([P, late_bytes_width], U8, name="late_bytes", offset=0, align_bytes=64)
-        late_words = ring.tile([P, 2 * (S - C) + 640], U32, name="late_words", offset=late_bytes_width, align_bytes=64)
+        dhs = [stage1(0)]
+        late_words = sb("late_words_sb", [P, sum(size for j0, size, s in LATE_GATHERS)], U32, "late_words")
         at = 0
         for j0, size, s in LATE_GATHERS:
-            if s is None:
-                gather_bytes(late_bytes[:], j0)
-            else:
-                gather_words(late_words[:, at:at + size], j0, s)
-                at += size
+            gather_words(late_words[:, at:at + size], j0, s)
+            at += size
+        dhs.append(stage1(P))
 
         dhts = []
         for n, (j0, size) in enumerate(UNITS):

@@ -22,12 +22,9 @@ MULT = mybir.AluOpType.mult
 
 WB_FIRST_ROW, WB_REST_ROW, WT_ROW, WA_ROW = 0, 4, 8, 12
 UNITS = [(0, 256), (256, 256), (512, 256), (768, 128), (896, 128)]
-LATE_GATHERS = [(128, 128, 1), (128, 128, 2), (384, 256, 0), (256, 256, 1), (256, 256, 2), (640, 384, 0), (512, 256, 1), (512, 256, 2),
-                (768, 256, 1), (768, 128, 2), (896, 128, 2)]
-TURNED_SUMS = [(0, 0)]
-FUSED_SUMS = [(0, 256, 256), (1, 0, 512)]
-SUM_BANKS = ((5, 2, 3), (7, 1, 4))
-WARM_PASSES = 2
+LATE_GATHERS = [(512, 256, 1), (512, 256, 2), (768, 256, 0), (768, 256, 1), (768, 128, 2), (896, 128, 2)]
+FUSED_SUMS = [(0, 0, 256), (0, 256, 256), (1, 0, 512)]
+WARM_PASSES = 6
 TURN_BANKS = (2, 4, 6, 0, 1)
 
 
@@ -52,7 +49,7 @@ def tile_moe_adb_none_kernel(
         wb_s_rest = sb("wb_s_rest", [P, (E - 1) * PASSES, H], U8)
         wa_s = sb("wa_s", [P, E, K], U8)
         wt_s = sb("wt_s", [P, PASSES, K], U8)
-        gate_rows = sb("gate_rows", [P, P], F32)
+        gate_rows = sb("gate_rows", [P, P], F32, "second_words")
         gate_cols = sb("gate_cols", [P, S // P], F32)
         ident = sb("ident", [P, P], F32)
 
@@ -112,12 +109,6 @@ def tile_moe_adb_none_kernel(
                 load_scales(nc.sync, wb_s_rest, WB_REST_ROW, wbs_hbm[:, PASSES:E * PASSES, :])
         wb_s = ([wb_s_first[WB_FIRST_ROW:P, s, :] for s in range(PASSES)]
                 + [wb_s_rest[WB_REST_ROW:P, a, :] for a in range((E - 1) * PASSES)])
-        load_scales(nc.sync, wa_s, WA_ROW, was_hbm)
-        wa_w = load_words(parts[-2], wa_hbm)
-        load_scales(nc.sync, wt_s, WT_ROW, wts_hbm)
-        wt_w = load_words(parts[-1], wt_hbm)
-        nc.sync.dma_start(pos_sb[0][:], pos1)
-        nc.sync.dma_start(pos_sb[1][:], pos2)
 
         def bank(n, shape):
             return psum.tile(shape, F32, name="bank%d" % n, tag="bank%d" % n)
@@ -126,7 +117,6 @@ def tile_moe_adb_none_kernel(
         nc.tensor.transpose(gate_turned[:], gate_rows[:], ident[:])
         nc.scalar.activation(gate_cols[:], gate_turned[:, 0:S // P], COPY)
 
-        first_words = sb("first_words", [P, P], U32, "late_words")
         g_s, g_w = {}, {}
 
         def gather_bytes(tile, j0):
@@ -141,20 +131,29 @@ def tile_moe_adb_none_kernel(
             for j in range(j0, j0 + size, P):
                 g_w[(j, s)] = tile[:, j - j0:j - j0 + P]
 
-        gather_words(first_words[:], 0, 0)
-        early_words = sb("early0", [P, 256], U32)
-        early_bytes = sb("early_s0", [P, C], U8)
-        gather_words(early_words[:], 128, 0)
-        gather_words(sb("early2", [P, P], U32)[:], 0, 1)
-        gather_words(sb("early3", [P, P], U32)[:], 0, 2)
-        gather_bytes(early_bytes[:], 0)
-        gather_bytes(sb("early_s1", [P, 384], U8)[:], C)
-        gather_bytes(sb("early_s2", [P, 384], U8)[:], C + 384)
+        next0 = sb("next0", [P, C], U32)
+        gather_words(next0[:], P, 0)
+        gather_words(sb("first0", [P, P], U32, "late_bytes")[:], 0, 0)
+        gather_words(sb("first1", [P, P], U32, "late_words")[:], 0, 1)
+        gather_words(sb("first2", [P, P], U32)[:], 0, 2)
+        gather_bytes(sb("early_s0", [P, P], U8)[:], 0)
+        gather_bytes(sb("early_s1", [P, 3 * P], U8)[:], P)
+        second_words = sb("second_words_sb", [P, PASSES, 3 * P], U32, "second_words")
+        gather_words(second_words[:, 1, :], P, 1)
+        gather_words(second_words[:, 2, :], P, 2)
+        gather_words(second_words[:, 0, :], 3 * P, 0)
 
         warm = bank(5, [P, C])
         for n in range(WARM_PASSES):
-            nc.tensor.matmul_mx(out=warm[:], lhsT=early_words[:, 0:P].bitcast(X4), lhsT_scale=early_bytes[:, 0:P],
-                                rhs=early_words[:].bitcast(X4), rhs_scale=early_bytes[:], start=True, stop=True)
+            nc.tensor.matmul_mx(out=warm[:], lhsT=next0[:, 0:P].bitcast(X4), lhsT_scale=wt_s[WT_ROW:P, 0, 0:P],
+                                rhs=next0[:].bitcast(X4), rhs_scale=wt_s[WT_ROW:P, 0, :], start=True, stop=True)
+
+        load_scales(nc.sync, wt_s, WT_ROW, wts_hbm)
+        wt_w = load_words(parts[-1], wt_hbm)
+        load_scales(nc.sync, wa_s, WA_ROW, was_hbm)
+        wa_w = load_words(parts[-2], wa_hbm)
+        nc.sync.dma_start(pos_sb[0][:], pos1)
+        nc.sync.dma_start(pos_sb[1][:], pos2)
 
         def stage1(j):
             e = j // C
@@ -194,13 +193,15 @@ def tile_moe_adb_none_kernel(
             copy(dht[:], turned[:, 0:2 * len(dhs), :].rearrange("p (m u) j -> p m j u", u=2))
             return dht
 
-        dhs = [stage1(0)]
+        dhs = [stage1(0), stage1(P)]
+        late_bytes = sb("late_bytes_sb", [P, 2 * C], U8, "late_bytes")
+        gather_bytes(late_bytes[:, 0:3 * P], 2 * C)
+        gather_bytes(late_bytes[:, 3 * P:4 * P], S - P)
         late_words = sb("late_words_sb", [P, sum(size for j0, size, s in LATE_GATHERS)], U32, "late_words")
         at = 0
         for j0, size, s in LATE_GATHERS:
             gather_words(late_words[:, at:at + size], j0, s)
             at += size
-        dhs.append(stage1(P))
 
         dhts = []
         for n, (j0, size) in enumerate(UNITS):
@@ -210,19 +211,20 @@ def tile_moe_adb_none_kernel(
             dhts.append(turn(n, dhs))
             dhs = ahead
 
-        def frozen(h, b):
-            acc = bank(b, [P, T])
+        base = [sb("base_sb%d" % h, [P, T], F32) for h in range(2)]
+
+        def frozen(h, t0, size, b):
+            acc = bank(b, [P, size])
             for s in range(PASSES):
                 nc.tensor.matmul_mx(
                     out=acc[:],
                     lhsT=wt_w[s][:, h * P:(h + 1) * P].bitcast(X4),
                     lhsT_scale=wt_s[WT_ROW:P, s, h * P:(h + 1) * P],
-                    rhs=dy_w[s].bitcast(X4), rhs_scale=dy_s[4 * s:P, :],
+                    rhs=dy_w[s][:, t0:t0 + size].bitcast(X4), rhs_scale=dy_s[4 * s:P, t0:t0 + size],
                     start=(s == 0), stop=(s == PASSES - 1),
                 )
-            base = sb("base_sb%d" % h, [P, T], F32)
-            nc.scalar.copy(base[:], acc[:])
-            return base
+            for at in range(0, size, C):
+                nc.scalar.copy(base[h][:, t0 + at:t0 + at + C], acc[:, at:at + C])
 
         dx = [sb("dx%d" % h, [P, S], F32) for h in range(2)]
         codes, planes = [], []
@@ -247,41 +249,23 @@ def tile_moe_adb_none_kernel(
                 )
             copy(dx[h][:, first:first + width], acc[:])
 
+        frozen(0, 0, C, 7)
         stage2(0, (0, 1), 2, nc.scalar.copy)
-        stage2(0, (2,), 6, nc.scalar.copy)
-        stage2(0, (3,), 7, nc.vector.tensor_copy)
-        stage2(0, (4,), 1, nc.vector.tensor_copy)
-        base = [frozen(0, 0)]
-        stage2(1, (0, 1), 3, nc.scalar.copy)
-        stage2(1, (2, 3, 4), 4, nc.scalar.copy)
-        base.append(frozen(1, 6))
-
-        for n, (h, t0) in enumerate(TURNED_SUMS):
-            cols = slice(t0 // 16, (t0 + C) // 16)
-            picked = [sb("picked%d_%d" % (n, r), [P, C], F32) for r in range(2)]
-            for r in range(2):
-                nc.vector.tensor_copy(picked[r][:], dx[h][:].indirect(pos_sb[r][:, cols]))
-            summed = [bank(SUM_BANKS[n][m], [P, P]) for m in range(2)]
-            for a, term in enumerate((base[h][:, t0:t0 + C], picked[0][:], picked[1][:])):
-                for m in range(2):
-                    nc.tensor.matmul(summed[m][:], term[:, m * P:(m + 1) * P], ident[:], start=(a == 0), stop=(a == 2), is_transpose=True)
-            sum_sb = sb("sum%d" % n, [P, 2, P], F32)
-            back = bank(SUM_BANKS[n][2], [P, 2, P])
-            for m in range(2):
-                nc.scalar.copy(sum_sb[:, m, :], summed[m][:])
-                nc.tensor.transpose(back[:, m, :], sum_sb[:, m, :], ident[:])
-            total = sb("total%d" % n, [P, C], F32)
-            nc.scalar.copy(total[:].rearrange("k (m t) -> k m t", t=P), back[:])
-            nc.scalar.dma_start(out=out[h * P:(h + 1) * P, t0:t0 + C], in_=total[:])
+        stage2(0, (2,), 3, nc.scalar.copy)
+        stage2(0, (3,), 4, nc.vector.tensor_copy)
+        stage2(0, (4,), 5, nc.vector.tensor_copy)
+        frozen(0, C, C, 4)
+        stage2(1, (0, 1), 2, nc.scalar.copy)
+        stage2(1, (2, 3, 4), 5, nc.scalar.copy)
+        frozen(1, 0, T, 3)
 
         for h, t0, size in FUSED_SUMS:
             half = size // 2
-            part = sb("part%d" % h, [P, size], F32)
-            last = [sb("last%d_%d" % (h, n), [P, half], F32) for n in range(2)]
-            cols = [slice((t0 + n * half) // 16, (t0 + (n + 1) * half) // 16) for n in range(2)]
-            for n in range(2):
-                nc.vector.tensor_tensor(part[:, n * half:(n + 1) * half], dx[h][:].indirect(pos_sb[0][:, cols[n]]),
-                                        base[h][:, t0 + n * half:t0 + (n + 1) * half], ADD)
-            for n in range(2):
-                nc.vector.tensor_tensor(last[n][:], dx[h][:].indirect(pos_sb[1][:, cols[n]]), part[:, n * half:(n + 1) * half], ADD)
-                nc.sync.dma_start(out=out[h * P:(h + 1) * P, t0 + n * half:t0 + (n + 1) * half], in_=last[n][:])
+            part = sb("part%d_%d" % (h, t0), [P, size], F32)
+            total = sb("total%d_%d" % (h, t0), [P, size], F32)
+            for r, (dst, term) in enumerate(((part[:], base[h][:, t0:t0 + size]), (total[:], part[:]))):
+                for at in (0, half):
+                    offsets = pos_sb[r][:, (t0 + at) // 16:(t0 + at + half) // 16]
+                    nc.vector.tensor_tensor(dst[:, at:at + half], dx[h][:].indirect(offsets), term[:, at:at + half], ADD)
+            for at in range(0, size, C):
+                nc.sync.dma_start(out=out[h * P:(h + 1) * P, t0 + at:t0 + at + C], in_=total[:, at:at + C])

@@ -22,9 +22,9 @@ MULT = mybir.AluOpType.mult
 
 WB_FIRST_ROW, WB_REST_ROW, WT_ROW, WA_ROW = 0, 4, 8, 12
 UNITS = [(0, 256), (256, 256), (512, 256), (768, 128), (896, 128)]
-LATE_GATHERS = [(512, 256, 1), (512, 256, 2), (768, 256, 0), (768, 256, 1), (768, 128, 2), (896, 128, 2)]
+LATE_GATHERS = [(512, 256, 1), (512, 256, 2), (896, 128, 0), (768, 256, 1), (768, 128, 2), (896, 128, 2)]
 FUSED_SUMS = [(0, 0, 256), (0, 256, 256), (1, 0, 512)]
-WARM_PASSES = 6
+WARM_PASSES = 4
 TURN_BANKS = (2, 4, 6, 0, 1)
 
 
@@ -45,8 +45,8 @@ def tile_moe_adb_none_kernel(
 
         dy_first = sb("dy_first", [P, T], U32)
         dy_s = sb("dy_s", [P, T], U8)
-        wb_s_first = sb("wb_s_first", [P, PASSES, H], U8)
-        wb_s_rest = sb("wb_s_rest", [P, (E - 1) * PASSES, H], U8)
+        wb_s_first = sb("wb_s_first", [P, 2 * PASSES, H], U8)
+        wb_s_rest = sb("wb_s_rest", [P, 2 * PASSES, H], U8)
         wa_s = sb("wa_s", [P, E, K], U8)
         wt_s = sb("wt_s", [P, PASSES, K], U8)
         gate_rows = sb("gate_rows", [P, P], F32, "second_words")
@@ -104,11 +104,11 @@ def tile_moe_adb_none_kernel(
             wb_w.extend(load_words(parts[n], wb_hbm[:, a0:a1, :]))
             if n == 0:
                 nc.sync.dma_start(out=gate_rows[0:S // P, :], in_=gate.rearrange("r (c p) -> (r c) p", p=P)[0:S // P, :])
-                load_scales(nc.sync, wb_s_first, WB_FIRST_ROW, wbs_hbm[:, 0:PASSES, :])
+                load_scales(nc.sync, wb_s_first, WB_FIRST_ROW, wbs_hbm[:, 0:2 * PASSES, :])
             if n == 1:
-                load_scales(nc.sync, wb_s_rest, WB_REST_ROW, wbs_hbm[:, PASSES:E * PASSES, :])
-        wb_s = ([wb_s_first[WB_FIRST_ROW:P, s, :] for s in range(PASSES)]
-                + [wb_s_rest[WB_REST_ROW:P, a, :] for a in range((E - 1) * PASSES)])
+                load_scales(nc.sync, wb_s_rest, WB_REST_ROW, wbs_hbm[:, 2 * PASSES:E * PASSES, :])
+        wb_s = ([wb_s_first[WB_FIRST_ROW:P, s, :] for s in range(2 * PASSES)]
+                + [wb_s_rest[WB_REST_ROW:P, a, :] for a in range(2 * PASSES)])
 
         def bank(n, shape):
             return psum.tile(shape, F32, name="bank%d" % n, tag="bank%d" % n)
@@ -131,22 +131,23 @@ def tile_moe_adb_none_kernel(
             for j in range(j0, j0 + size, P):
                 g_w[(j, s)] = tile[:, j - j0:j - j0 + P]
 
-        next0 = sb("next0", [P, C], U32)
+        next0 = sb("next0", [P, 3 * P], U32)
         gather_words(next0[:], P, 0)
         gather_words(sb("first0", [P, P], U32, "late_bytes")[:], 0, 0)
         gather_words(sb("first1", [P, P], U32, "late_words")[:], 0, 1)
         gather_words(sb("first2", [P, P], U32)[:], 0, 2)
-        gather_bytes(sb("early_s0", [P, P], U8)[:], 0)
-        gather_bytes(sb("early_s1", [P, 3 * P], U8)[:], P)
+        first_s = sb("first_s", [P, C], U8)
+        gather_bytes(first_s[:], 0)
+        gather_bytes(sb("second_s", [P, C], U8)[:], C)
         second_words = sb("second_words_sb", [P, PASSES, 3 * P], U32, "second_words")
         gather_words(second_words[:, 1, :], P, 1)
         gather_words(second_words[:, 2, :], P, 2)
-        gather_words(second_words[:, 0, :], 3 * P, 0)
+        gather_words(second_words[:, 0, :], 2 * C, 0)
 
         warm = bank(5, [P, C])
         for n in range(WARM_PASSES):
-            nc.tensor.matmul_mx(out=warm[:], lhsT=next0[:, 0:P].bitcast(X4), lhsT_scale=wt_s[WT_ROW:P, 0, 0:P],
-                                rhs=next0[:].bitcast(X4), rhs_scale=wt_s[WT_ROW:P, 0, :], start=True, stop=True)
+            nc.tensor.matmul_mx(out=warm[:], lhsT=next0[:, 0:P].bitcast(X4), lhsT_scale=first_s[:, 0:P],
+                                rhs=next0[:, 0:C].bitcast(X4), rhs_scale=first_s[:], start=True, stop=True)
 
         load_scales(nc.sync, wt_s, WT_ROW, wts_hbm)
         wt_w = load_words(parts[-1], wt_hbm)

@@ -24,7 +24,6 @@ WB_FIRST_ROW, WB_REST_ROW, WT_ROW, WA_ROW = 0, 4, 8, 12
 UNITS = [(0, 256), (256, 256), (512, 256), (768, 128), (896, 128)]
 LATE_GATHERS = [(512, 256, 1), (512, 256, 2), (896, 128, 0), (768, 256, 1), (768, 128, 2), (896, 128, 2)]
 FUSED_SUMS = [(0, 0, 256), (0, 256, 256), (1, 0, 512)]
-WARM_PASSES = 4
 TURN_BANKS = (2, 4, 6, 0, 1)
 
 
@@ -143,11 +142,6 @@ def tile_moe_adb_none_kernel(
         gather_words(second_words[:, 1, :], P, 1)
         gather_words(second_words[:, 2, :], P, 2)
         gather_words(second_words[:, 0, :], 2 * C, 0)
-
-        warm = bank(5, [P, C])
-        for n in range(WARM_PASSES):
-            nc.tensor.matmul_mx(out=warm[:], lhsT=next0[:, 0:P].bitcast(X4), lhsT_scale=first_s[:, 0:P],
-                                rhs=next0[:, 0:C].bitcast(X4), rhs_scale=first_s[:], start=True, stop=True)
 
         load_scales(nc.sync, wt_s, WT_ROW, wts_hbm)
         wt_w = load_words(parts[-1], wt_hbm)

@@ -21,10 +21,10 @@ ADD = mybir.AluOpType.add
 MULT = mybir.AluOpType.mult
 
 WB_FIRST_ROW, WB_REST_ROW, WT_ROW, WA_ROW = 0, 4, 8, 12
-UNITS = [(0, 256), (256, 256), (512, 256), (768, 128), (896, 128)]
+UNITS = [(0, 128), (128, 256), (384, 256), (640, 256), (896, 128)]
 LATE_GATHERS = [(512, 256, 1), (512, 256, 2), (896, 128, 0), (768, 256, 1), (768, 128, 2), (896, 128, 2)]
-FUSED_SUMS = [(0, 0, 256), (0, 256, 256), (1, 0, 512)]
-TURN_BANKS = (2, 4, 6, 0, 1)
+WARM_PASSES = 4
+TURN_BANKS = (2, 0, 3, 5, 4)
 
 
 def tile_moe_adb_none_kernel(
@@ -143,10 +143,15 @@ def tile_moe_adb_none_kernel(
         gather_words(second_words[:, 2, :], P, 2)
         gather_words(second_words[:, 0, :], 2 * C, 0)
 
-        load_scales(nc.sync, wt_s, WT_ROW, wts_hbm)
-        wt_w = load_words(parts[-1], wt_hbm)
+        warm = bank(5, [P, C])
+        for n in range(WARM_PASSES):
+            nc.tensor.matmul_mx(out=warm[:], lhsT=next0[:, 0:P].bitcast(X4), lhsT_scale=first_s[:, 0:P],
+                                rhs=next0[:, 0:C].bitcast(X4), rhs_scale=first_s[:], start=True, stop=True)
+
         load_scales(nc.sync, wa_s, WA_ROW, was_hbm)
         wa_w = load_words(parts[-2], wa_hbm)
+        load_scales(nc.sync, wt_s, WT_ROW, wts_hbm)
+        wt_w = load_words(parts[-1], wt_hbm)
         nc.sync.dma_start(pos_sb[0][:], pos1)
         nc.sync.dma_start(pos_sb[1][:], pos2)
 
@@ -184,7 +189,7 @@ def tile_moe_adb_none_kernel(
                 for u in range(2):
                     nc.tensor.transpose(turned[:, 2 * m + u, :], pairs[:, u * P:(u + 1) * P], ident[:])
             dht = sb("dht%d" % n, [P, len(dhs), P, 2], F32)
-            copy = nc.vector.tensor_copy if n == 2 else nc.scalar.copy
+            copy = nc.vector.tensor_copy if n == len(UNITS) - 1 else nc.scalar.copy
             copy(dht[:], turned[:, 0:2 * len(dhs), :].rearrange("p (m u) j -> p m j u", u=2))
             return dht
 
@@ -199,14 +204,12 @@ def tile_moe_adb_none_kernel(
             at += size
 
         dhts = []
-        for n, (j0, size) in enumerate(UNITS):
-            if n + 1 < len(UNITS):
-                j1, size1 = UNITS[n + 1]
-                ahead = [stage1(j) for j in range(j1, j1 + size1, P)]
-            dhts.append(turn(n, dhs))
-            dhs = ahead
-
-        base = [sb("base_sb%d" % h, [P, T], F32) for h in range(2)]
+        for j in range(2 * P, S, P):
+            dhs.append(stage1(j))
+            while len(dhts) < len(UNITS) - 1 and sum(UNITS[len(dhts)]) <= j:
+                j0, size = UNITS[len(dhts)]
+                dhts.append(turn(len(dhts), dhs[j0 // P:(j0 + size) // P]))
+        dhts.append(turn(len(dhts), dhs[-1:]))
 
         def frozen(h, t0, size, b):
             acc = bank(b, [P, size])
@@ -218,49 +221,64 @@ def tile_moe_adb_none_kernel(
                     rhs=dy_w[s][:, t0:t0 + size].bitcast(X4), rhs_scale=dy_s[4 * s:P, t0:t0 + size],
                     start=(s == 0), stop=(s == PASSES - 1),
                 )
-            for at in range(0, size, C):
-                nc.scalar.copy(base[h][:, t0 + at:t0 + at + C], acc[:, at:at + C])
+            return acc
 
         dx = [sb("dx%d" % h, [P, S], F32) for h in range(2)]
-        codes, planes = [], []
+        codes = sb("dh_w", [P, S], U32)
+        planes = sb("dh_s", [P, S], U8)
         for n, (j0, size) in enumerate(UNITS):
-            codes.append(sb("dh_w%d" % n, [P, size], U32))
-            planes.append(sb("dh_s%d" % n, [P, size], U8))
-            nc.vector.quantize_mx(out=codes[n][:].bitcast(X4), scales=planes[n][:],
+            nc.vector.quantize_mx(out=codes[:, j0:j0 + size].bitcast(X4), scales=planes[:, j0:j0 + size],
                                   in_=dhts[n][:].rearrange("p m j u -> p (m j u)").bitcast(BF16))
 
-        def stage2(h, units, b, copy):
-            first = UNITS[units[0]][0]
-            width = sum(UNITS[n][1] for n in units)
-            acc = bank(b, [P, width])
-            for n in units:
-                j0, size = UNITS[n]
+        def stage2(h, first, sizes, b, copy):
+            acc = bank(b, [P, sum(sizes)])
+            j0 = first
+            for size in sizes:
                 nc.tensor.matmul_mx(
                     out=acc[:, j0 - first:j0 - first + size],
                     lhsT=wa_w[j0 // C][:, h * P:(h + 1) * P].bitcast(X4),
                     lhsT_scale=wa_s[WA_ROW:P, j0 // C, h * P:(h + 1) * P],
-                    rhs=codes[n][:].bitcast(X4), rhs_scale=planes[n][:],
+                    rhs=codes[:, j0:j0 + size].bitcast(X4), rhs_scale=planes[:, j0:j0 + size],
                     start=True, stop=True,
                 )
-            copy(dx[h][:, first:first + width], acc[:])
+                j0 += size
+            copy(dx[h][:, first:j0], acc[:])
 
-        frozen(0, 0, C, 7)
-        stage2(0, (0, 1), 2, nc.scalar.copy)
-        stage2(0, (2,), 3, nc.scalar.copy)
-        stage2(0, (3,), 4, nc.vector.tensor_copy)
-        stage2(0, (4,), 5, nc.vector.tensor_copy)
-        frozen(0, C, C, 4)
-        stage2(1, (0, 1), 2, nc.scalar.copy)
-        stage2(1, (2, 3, 4), 5, nc.scalar.copy)
-        frozen(1, 0, T, 3)
+        copies = (nc.scalar.copy, nc.vector.tensor_copy)
+        for first, sizes, banks in ((0, (C, C), (2, 3)), (2 * C, (C, P), (0, 6)), (S - P, (P,), (7, 1))):
+            for h in range(2):
+                stage2(h, first, sizes, banks[h], copies[h])
+        base_first = sb("base_first", [P, C], F32)
+        nc.scalar.copy(base_first[:], frozen(0, 0, C, 5)[:])
+        base = {(0, C): frozen(0, C, C, 4)[:]}
+        lower = frozen(1, 0, T, 7)
+        for t0 in (0, C):
+            base[(1, t0)] = lower[:, t0:t0 + C]
 
-        for h, t0, size in FUSED_SUMS:
-            half = size // 2
-            part = sb("part%d_%d" % (h, t0), [P, size], F32)
-            total = sb("total%d_%d" % (h, t0), [P, size], F32)
-            for r, (dst, term) in enumerate(((part[:], base[h][:, t0:t0 + size]), (total[:], part[:]))):
-                for at in (0, half):
-                    offsets = pos_sb[r][:, (t0 + at) // 16:(t0 + at + half) // 16]
-                    nc.vector.tensor_tensor(dst[:, at:at + half], dx[h][:].indirect(offsets), term[:, at:at + half], ADD)
-            for at in range(0, size, C):
-                nc.sync.dma_start(out=out[h * P:(h + 1) * P, t0 + at:t0 + at + C], in_=total[:, at:at + C])
+        def picked(h, r, t0, size):
+            return dx[h][:].indirect(pos_sb[r][:, t0 // 16:(t0 + size) // 16])
+
+        def fetch(h, r, t0, size):
+            tile = sb("got%d_%d_%d" % (h, r, t0), [P, size], F32)
+            nc.scalar.activation(tile[:], picked(h, r, t0, size), COPY)
+            return tile[:]
+
+        def add(name, h, t0, size, in0, in1):
+            tile = sb("%s%d_%d" % (name, h, t0), [P, size], F32)
+            nc.vector.tensor_tensor(tile[:], in0, in1, ADD)
+            return tile[:]
+
+        def with_base(h, t0, size):
+            return add("part", h, t0, size, base[(h, t0)], fetch(h, 0, t0, size))
+
+        def finish(h, t0, size, second, part):
+            nc.sync.dma_start(out=out[h * P:(h + 1) * P, t0:t0 + size], in_=add("total", h, t0, size, second, part))
+
+        quarters = (0, P)
+        fused = [add("part", 0, t0, P, picked(0, 0, t0, P), base_first[:, t0:t0 + P]) for t0 in quarters]
+        for t0, part in zip(quarters, fused):
+            finish(0, t0, P, picked(0, 1, t0, P), part)
+        finish(0, C, C, picked(0, 1, C, C), with_base(0, C, C))
+        for t0 in (0, C):
+            part = with_base(1, t0, C)
+            finish(1, t0, C, fetch(1, 1, t0, C), part)

@@ -21,10 +21,12 @@ ADD = mybir.AluOpType.add
 MULT = mybir.AluOpType.mult
 
 WB_FIRST_ROW, WB_REST_ROW, WT_ROW, WA_ROW = 0, 4, 8, 12
-UNITS = [(0, 128), (128, 256), (384, 256), (640, 256), (896, 128)]
-LATE_GATHERS = [(512, 256, 1), (512, 256, 2), (896, 128, 0), (768, 256, 1), (768, 128, 2), (896, 128, 2)]
-WARM_PASSES = 4
+WB_LOADS = ((0, 3), (3, 6), (6, 9), (9, 11), (11, 12))
+TURNS = ((0, P), (P, C), (C + P, C), (2 * C + P, C), (S - P, P))
 TURN_BANKS = (2, 0, 3, 5, 4)
+GATE_BANK, WARM_BANK = 7, 5
+LAST_TILE_BANKS = (7, 1)
+WARM_PASSES = 4
 
 
 def tile_moe_adb_none_kernel(
@@ -36,8 +38,11 @@ def tile_moe_adb_none_kernel(
         keep = ctx.enter_context(tc.tile_pool(name="keep", bufs=1))
         psum = ctx.enter_context(tc.psum_pool(name="psum", bufs=1))
 
-        def sb(name, shape, dtype, slot=None):
-            return keep.tile(shape, dtype, name=name, tag=slot or name, align_bytes=64)
+        def sb(name, shape, dtype, room=None):
+            return keep.tile(shape, dtype, name=name, tag=room or name, align_bytes=64)
+
+        def bank(n, shape):
+            return psum.tile(shape, F32, name="bank%d" % n, tag="bank%d" % n)
 
         offs_sb = keep.tile([P, S // 16], U16, name="offs_sb")
         pos_sb = [keep.tile([P, T // 16], U16, name="pos%d_sb" % r) for r in range(2)]
@@ -55,10 +60,8 @@ def tile_moe_adb_none_kernel(
         nc.gpsimd.memset(dy_s[:].bitcast(I32), 0)
         nc.gpsimd.memset(gate_rows[:], 0.0)
         make_identity(nc, ident[:])
-        nc.vector.memset(wb_s_first[:].bitcast(I32), 0)
-        nc.vector.memset(wb_s_rest[:].bitcast(I32), 0)
-        nc.vector.memset(wa_s[:].bitcast(I32), 0)
-        nc.vector.memset(wt_s[:].bitcast(I32), 0)
+        for plane in (wb_s_first, wb_s_rest, wa_s, wt_s):
+            nc.vector.memset(plane[:].bitcast(I32), 0)
         dy_rest = sb("dy_rest", [P, PASSES - 1, T], U32)
         dy_w = [dy_first[:]] + [dy_rest[:, s, :] for s in range(PASSES - 1)]
 
@@ -74,92 +77,87 @@ def tile_moe_adb_none_kernel(
         def load_dy_scales(queue, q):
             queue.dma_start(out=dy_s[32 * q:32 * q + 4 * PASSES, :].bitcast(I32), in_=dys_hbm[:, 4 * q:4 * q + 4, :])
 
-        def load_scales(queue, tile, row0, hbm):
+        def load_scales(plane, row, hbm):
             for r in range(4):
-                queue.dma_start(out=tile[row0 + r:P:32, :, :].bitcast(I32), in_=hbm[r:16:4])
-
-        nc.sync.dma_start(offs_sb[:], offs)
-        nc.sync.dma_start(out=dy_first[:].bitcast(I32), in_=dy_hbm[:, 0, :])
-        nc.sync.dma_start(out=dy_rest[:].bitcast(I32), in_=dy_hbm[:, 1:PASSES, :])
-        load_dy_scales(nc.scalar, 0)
-        load_dy_scales(nc.sync, 2)
-        load_dy_scales(nc.scalar, 1)
-        load_dy_scales(nc.sync, 3)
-
-        def carve(name, widths):
-            tile = sb(name, [P, sum(widths)], U32)
-            ends = [sum(widths[:n + 1]) for n in range(len(widths))]
-            return [tile[:, end - width:end] for width, end in zip(widths, ends)]
+                nc.sync.dma_start(out=plane[row + r:P:32, :, :].bitcast(I32), in_=hbm[r:16:4])
 
         def load_words(dst, hbm):
             view = dst.rearrange("p (a c) -> p a c", a=hbm.shape[1])
             nc.sync.dma_start(out=view.bitcast(I32), in_=hbm)
             return [view[:, a, :] for a in range(hbm.shape[1])]
 
-        runs = [(0, 3), (3, 6), (6, 9), (9, 11), (11, 12)]
-        parts = carve("late_loads", [(a1 - a0) * H for a0, a1 in runs] + [E * K, PASSES * K])
+        nc.sync.dma_start(offs_sb[:], offs)
+        nc.sync.dma_start(out=dy_first[:].bitcast(I32), in_=dy_hbm[:, 0, :])
+        nc.sync.dma_start(out=dy_rest[:].bitcast(I32), in_=dy_hbm[:, 1:PASSES, :])
+        for q in range(2):
+            load_dy_scales(nc.scalar, q)
+            load_dy_scales(nc.sync, q + 2)
+
+        wb_columns = E * PASSES * H
+        weights = sb("weights", [P, wb_columns + E * K + PASSES * K], U32)
         wb_w = []
-        for n, (a0, a1) in enumerate(runs):
-            wb_w.extend(load_words(parts[n], wb_hbm[:, a0:a1, :]))
+        for n, (a0, a1) in enumerate(WB_LOADS):
+            wb_w.extend(load_words(weights[:, a0 * H:a1 * H], wb_hbm[:, a0:a1, :]))
             if n == 0:
                 nc.sync.dma_start(out=gate_rows[0:S // P, :], in_=gate.rearrange("r (c p) -> (r c) p", p=P)[0:S // P, :])
-                load_scales(nc.sync, wb_s_first, WB_FIRST_ROW, wbs_hbm[:, 0:2 * PASSES, :])
+                load_scales(wb_s_first, WB_FIRST_ROW, wbs_hbm[:, 0:2 * PASSES, :])
             if n == 1:
-                load_scales(nc.sync, wb_s_rest, WB_REST_ROW, wbs_hbm[:, 2 * PASSES:E * PASSES, :])
-        wb_s = ([wb_s_first[WB_FIRST_ROW:P, s, :] for s in range(2 * PASSES)]
+                load_scales(wb_s_rest, WB_REST_ROW, wbs_hbm[:, 2 * PASSES:E * PASSES, :])
+        wb_s = ([wb_s_first[WB_FIRST_ROW:P, a, :] for a in range(2 * PASSES)]
                 + [wb_s_rest[WB_REST_ROW:P, a, :] for a in range(2 * PASSES)])
 
-        def bank(n, shape):
-            return psum.tile(shape, F32, name="bank%d" % n, tag="bank%d" % n)
-
-        gate_turned = bank(7, [P, P])
+        gate_turned = bank(GATE_BANK, [P, P])
         nc.tensor.transpose(gate_turned[:], gate_rows[:], ident[:])
         nc.scalar.activation(gate_cols[:], gate_turned[:, 0:S // P], COPY)
 
-        g_s, g_w = {}, {}
+        got_bytes, got_words = {}, {}
 
-        def gather_bytes(tile, j0):
-            size = tile.shape[1]
-            nc.vector.tensor_copy(tile, dy_s[:].indirect(offs_sb[:, j0 // 16:(j0 + size) // 16]))
+        def gather_bytes(dst, j0):
+            size = dst.shape[1]
+            nc.vector.tensor_copy(dst, dy_s[:].indirect(offs_sb[:, j0 // 16:(j0 + size) // 16]))
             for j in range(j0, j0 + size, P):
-                g_s[j] = tile[:, j - j0:j - j0 + P]
+                got_bytes[j] = dst[:, j - j0:j - j0 + P]
 
-        def gather_words(tile, j0, s):
-            size = tile.shape[1]
-            nc.vector.tensor_copy(tile, dy_w[s].indirect(offs_sb[:, j0 // 16:(j0 + size) // 16]))
+        def gather_words(dst, j0, s):
+            size = dst.shape[1]
+            nc.vector.tensor_copy(dst, dy_w[s].indirect(offs_sb[:, j0 // 16:(j0 + size) // 16]))
             for j in range(j0, j0 + size, P):
-                g_w[(j, s)] = tile[:, j - j0:j - j0 + P]
+                got_words[(j, s)] = dst[:, j - j0:j - j0 + P]
 
-        next0 = sb("next0", [P, 3 * P], U32)
-        gather_words(next0[:], P, 0)
-        gather_words(sb("first0", [P, P], U32, "late_bytes")[:], 0, 0)
-        gather_words(sb("first1", [P, P], U32, "late_words")[:], 0, 1)
-        gather_words(sb("first2", [P, P], U32)[:], 0, 2)
-        first_s = sb("first_s", [P, C], U8)
-        gather_bytes(first_s[:], 0)
-        gather_bytes(sb("second_s", [P, C], U8)[:], C)
-        second_words = sb("second_words_sb", [P, PASSES, 3 * P], U32, "second_words")
-        gather_words(second_words[:, 1, :], P, 1)
-        gather_words(second_words[:, 2, :], P, 2)
-        gather_words(second_words[:, 0, :], 2 * C, 0)
+        def gather_group(name, pieces):
+            group = sb(name + "_sb", [P, sum(size for j0, size, s in pieces)], U32, name)
+            at = 0
+            for j0, size, s in pieces:
+                gather_words(group[:, at:at + size], j0, s)
+                at += size
 
-        warm = bank(5, [P, C])
+        early_words = sb("early_words", [P, C], U32)
+        gather_words(early_words[:], P, 0)
+        gather_words(sb("tile0_pass0", [P, P], U32, "late_bytes")[:], 0, 0)
+        gather_words(sb("adapter0_pass1", [P, C], U32, "late_words")[:], 0, 1)
+        gather_words(sb("tile0_pass2", [P, P], U32)[:], 0, 2)
+        first_bytes = sb("first_bytes", [P, C], U8)
+        gather_bytes(first_bytes[:], 0)
+        gather_bytes(sb("second_bytes", [P, C], U8)[:], C)
+        gather_group("second_words", ((P, P, 2), (C + P, P, 0), (C, C, 1), (C, C, 2), (2 * C, 3 * P, 0)))
+
+        warm = bank(WARM_BANK, [P, C])
         for n in range(WARM_PASSES):
-            nc.tensor.matmul_mx(out=warm[:], lhsT=next0[:, 0:P].bitcast(X4), lhsT_scale=first_s[:, 0:P],
-                                rhs=next0[:, 0:C].bitcast(X4), rhs_scale=first_s[:], start=True, stop=True)
+            nc.tensor.matmul_mx(out=warm[:], lhsT=early_words[:, 0:P].bitcast(X4), lhsT_scale=first_bytes[:, 0:P],
+                                rhs=early_words[:, 0:C].bitcast(X4), rhs_scale=first_bytes[:], start=True, stop=True)
 
-        load_scales(nc.sync, wa_s, WA_ROW, was_hbm)
-        wa_w = load_words(parts[-2], wa_hbm)
-        load_scales(nc.sync, wt_s, WT_ROW, wts_hbm)
-        wt_w = load_words(parts[-1], wt_hbm)
+        load_scales(wa_s, WA_ROW, was_hbm)
+        wa_w = load_words(weights[:, wb_columns:wb_columns + E * K], wa_hbm)
+        load_scales(wt_s, WT_ROW, wts_hbm)
+        wt_w = load_words(weights[:, wb_columns + E * K:wb_columns + E * K + PASSES * K], wt_hbm)
         nc.sync.dma_start(pos_sb[0][:], pos1)
         nc.sync.dma_start(pos_sb[1][:], pos2)
 
-        def stage1(j):
+        def first_product(j):
             e = j // C
             m = j // P
             dh = sb("dh%d" % m, [P, 2, P, 2], BF16)
-            banks = (7, 1) if j == S - P else (m,)
+            banks = LAST_TILE_BANKS if j == S - P else (m,)
             width = H // len(banks)
             accs = [bank(b, [P, width]) for b in banks]
             for s in range(PASSES):
@@ -167,8 +165,8 @@ def tile_moe_adb_none_kernel(
                     cols = slice(n * width, (n + 1) * width)
                     nc.tensor.matmul_mx(
                         out=acc[:],
-                        lhsT=g_w[(j, s)].bitcast(X4),
-                        lhsT_scale=g_s[j][4 * s:P, :],
+                        lhsT=got_words[(j, s)].bitcast(X4),
+                        lhsT_scale=got_bytes[j][4 * s:P, :],
                         rhs=wb_w[e * PASSES + s][:, cols].bitcast(X4),
                         rhs_scale=wb_s[e * PASSES + s][:, cols],
                         start=(s == 0), stop=(s == PASSES - 1),
@@ -182,34 +180,54 @@ def tile_moe_adb_none_kernel(
                     nc.vector.tensor_scalar(dst, src, gate_cols[:, m:m + 1], None, MULT)
             return dh
 
-        def turn(n, dhs):
+        def turn(n, tiles):
             turned = bank(TURN_BANKS[n], [P, 4, P])
-            for m, dh in enumerate(dhs):
+            for m, dh in enumerate(tiles):
                 pairs = dh[:].rearrange("j u p v -> j (u p v)").bitcast(F32)
                 for u in range(2):
                     nc.tensor.transpose(turned[:, 2 * m + u, :], pairs[:, u * P:(u + 1) * P], ident[:])
-            dht = sb("dht%d" % n, [P, len(dhs), P, 2], F32)
-            copy = nc.vector.tensor_copy if n == len(UNITS) - 1 else nc.scalar.copy
-            copy(dht[:], turned[:, 0:2 * len(dhs), :].rearrange("p (m u) j -> p m j u", u=2))
+            dht = sb("dht%d" % n, [P, len(tiles), P, 2], F32)
+            copy = nc.vector.tensor_copy if n == len(TURNS) - 1 else nc.scalar.copy
+            copy(dht[:], turned[:, 0:2 * len(tiles), :].rearrange("p (m u) j -> p m j u", u=2))
             return dht
 
-        dhs = [stage1(0), stage1(P)]
+        dhs = [first_product(0), first_product(P)]
+
         late_bytes = sb("late_bytes_sb", [P, 2 * C], U8, "late_bytes")
         gather_bytes(late_bytes[:, 0:3 * P], 2 * C)
         gather_bytes(late_bytes[:, 3 * P:4 * P], S - P)
-        late_words = sb("late_words_sb", [P, sum(size for j0, size, s in LATE_GATHERS)], U32, "late_words")
-        at = 0
-        for j0, size, s in LATE_GATHERS:
-            gather_words(late_words[:, at:at + size], j0, s)
-            at += size
+        gather_group("late_words", ((2 * C, C, 1), (2 * C, C, 2), (S - P, P, 0),
+                                    (3 * C, C, 1), (3 * C, P, 2), (S - P, P, 2)))
 
         dhts = []
         for j in range(2 * P, S, P):
-            dhs.append(stage1(j))
-            while len(dhts) < len(UNITS) - 1 and sum(UNITS[len(dhts)]) <= j:
-                j0, size = UNITS[len(dhts)]
+            dhs.append(first_product(j))
+            while len(dhts) < len(TURNS) - 1 and sum(TURNS[len(dhts)]) <= j:
+                j0, size = TURNS[len(dhts)]
                 dhts.append(turn(len(dhts), dhs[j0 // P:(j0 + size) // P]))
         dhts.append(turn(len(dhts), dhs[-1:]))
+
+        dx = [sb("dx%d" % h, [P, S], F32) for h in range(2)]
+        dh_codes = sb("dh_codes", [P, S], U32)
+        dh_scales = sb("dh_scales", [P, S], U8)
+        for n, (j0, size) in enumerate(TURNS):
+            nc.vector.quantize_mx(out=dh_codes[:, j0:j0 + size].bitcast(X4), scales=dh_scales[:, j0:j0 + size],
+                                  in_=dhts[n][:].rearrange("p m j u -> p (m j u)").bitcast(BF16))
+
+        def second_product(h, first, sizes, b):
+            acc = bank(b, [P, sum(sizes)])
+            j0 = first
+            for size in sizes:
+                nc.tensor.matmul_mx(
+                    out=acc[:, j0 - first:j0 - first + size],
+                    lhsT=wa_w[j0 // C][:, h * P:(h + 1) * P].bitcast(X4),
+                    lhsT_scale=wa_s[WA_ROW:P, j0 // C, h * P:(h + 1) * P],
+                    rhs=dh_codes[:, j0:j0 + size].bitcast(X4), rhs_scale=dh_scales[:, j0:j0 + size],
+                    start=True, stop=True,
+                )
+                j0 += size
+            copy = nc.vector.tensor_copy if h else nc.scalar.copy
+            copy(dx[h][:, first:j0], acc[:])
 
         def frozen(h, t0, size, b):
             acc = bank(b, [P, size])
@@ -223,62 +241,36 @@ def tile_moe_adb_none_kernel(
                 )
             return acc
 
-        dx = [sb("dx%d" % h, [P, S], F32) for h in range(2)]
-        codes = sb("dh_w", [P, S], U32)
-        planes = sb("dh_s", [P, S], U8)
-        for n, (j0, size) in enumerate(UNITS):
-            nc.vector.quantize_mx(out=codes[:, j0:j0 + size].bitcast(X4), scales=planes[:, j0:j0 + size],
-                                  in_=dhts[n][:].rearrange("p m j u -> p (m j u)").bitcast(BF16))
-
-        def stage2(h, first, sizes, b, copy):
-            acc = bank(b, [P, sum(sizes)])
-            j0 = first
-            for size in sizes:
-                nc.tensor.matmul_mx(
-                    out=acc[:, j0 - first:j0 - first + size],
-                    lhsT=wa_w[j0 // C][:, h * P:(h + 1) * P].bitcast(X4),
-                    lhsT_scale=wa_s[WA_ROW:P, j0 // C, h * P:(h + 1) * P],
-                    rhs=codes[:, j0:j0 + size].bitcast(X4), rhs_scale=planes[:, j0:j0 + size],
-                    start=True, stop=True,
-                )
-                j0 += size
-            copy(dx[h][:, first:j0], acc[:])
-
-        copies = (nc.scalar.copy, nc.vector.tensor_copy)
-        for first, sizes, banks in ((0, (C, C), (2, 3)), (2 * C, (C, P), (0, 6)), (S - P, (P,), (7, 1))):
+        for first, sizes, banks in ((0, (C, C), (2, 3)), (2 * C, (C, P), (0, 6)), (S - P, (P,), LAST_TILE_BANKS)):
             for h in range(2):
-                stage2(h, first, sizes, banks[h], copies[h])
+                second_product(h, first, sizes, banks[h])
+
         base_first = sb("base_first", [P, C], F32)
-        nc.scalar.copy(base_first[:], frozen(0, 0, C, 5)[:])
-        base = {(0, C): frozen(0, C, C, 4)[:]}
-        lower = frozen(1, 0, T, 7)
-        for t0 in (0, C):
-            base[(1, t0)] = lower[:, t0:t0 + C]
+        nc.scalar.copy(base_first[:], frozen(0, 0, C, TURN_BANKS[-2])[:])
+        base_second = frozen(0, C, C, TURN_BANKS[-1])
+        base_lower = frozen(1, 0, T, LAST_TILE_BANKS[0])
 
         def picked(h, r, t0, size):
             return dx[h][:].indirect(pos_sb[r][:, t0 // 16:(t0 + size) // 16])
 
-        def fetch(h, r, t0, size):
-            tile = sb("got%d_%d_%d" % (h, r, t0), [P, size], F32)
-            nc.scalar.activation(tile[:], picked(h, r, t0, size), COPY)
-            return tile[:]
+        def fetch(h, r, t0):
+            got = sb("got%d_%d_%d" % (h, r, t0), [P, C], F32)
+            nc.scalar.activation(got[:], picked(h, r, t0, C), COPY)
+            return got[:]
 
         def add(name, h, t0, size, in0, in1):
-            tile = sb("%s%d_%d" % (name, h, t0), [P, size], F32)
-            nc.vector.tensor_tensor(tile[:], in0, in1, ADD)
-            return tile[:]
-
-        def with_base(h, t0, size):
-            return add("part", h, t0, size, base[(h, t0)], fetch(h, 0, t0, size))
+            result = sb("%s%d_%d" % (name, h, t0), [P, size], F32)
+            nc.vector.tensor_tensor(result[:], in0, in1, ADD)
+            return result[:]
 
         def finish(h, t0, size, second, part):
             nc.sync.dma_start(out=out[h * P:(h + 1) * P, t0:t0 + size], in_=add("total", h, t0, size, second, part))
 
-        quarters = (0, P)
-        fused = [add("part", 0, t0, P, picked(0, 0, t0, P), base_first[:, t0:t0 + P]) for t0 in quarters]
-        for t0, part in zip(quarters, fused):
+        pieces = (0, P)
+        fused = [add("part", 0, t0, P, picked(0, 0, t0, P), base_first[:, t0:t0 + P]) for t0 in pieces]
+        for t0, part in zip(pieces, fused):
             finish(0, t0, P, picked(0, 1, t0, P), part)
-        finish(0, C, C, picked(0, 1, C, C), with_base(0, C, C))
+        finish(0, C, C, picked(0, 1, C, C), add("part", 0, C, C, base_second[:], fetch(0, 0, C)))
         for t0 in (0, C):
-            part = with_base(1, t0, C)
-            finish(1, t0, C, fetch(1, 1, t0, C), part)
+            part = add("part", 1, t0, C, base_lower[:, t0:t0 + C], fetch(1, 0, t0))
+            finish(1, t0, C, fetch(1, 1, t0), part)

@@ -21,11 +21,9 @@ ADD = mybir.AluOpType.add
 MULT = mybir.AluOpType.mult
 
 WB_FIRST_ROW, WB_REST_ROW, WT_ROW, WA_ROW = 0, 4, 8, 12
-WB_LOADS = ((0, 3), (3, 6), (6, 9), (9, 11), (11, 12))
-TURNS = ((0, P), (P, C), (C + P, C), (2 * C + P, C), (S - P, P))
-TURN_BANKS = (2, 0, 3, 5, 4)
-GATE_BANK, WARM_BANK = 7, 5
-LAST_TILE_BANKS = (7, 1)
+TILE_BANKS = ((0,), (1,), (2,), (3,), (4,), (5,), (6, 1), (7, 3))
+TURNS = ((0, 2, 2), (2, 2, 4), (4, 2, 6), (6, 1, 0), (7, 1, 5))
+GATE_BANK, WARM_BANK = 5, 5
 WARM_PASSES = 4
 
 
@@ -48,6 +46,8 @@ def tile_moe_adb_none_kernel(
         pos_sb = [keep.tile([P, T // 16], U16, name="pos%d_sb" % r) for r in range(2)]
 
         dy_first = sb("dy_first", [P, T], U32)
+        dy_rest = sb("dy_rest", [P, PASSES - 1, T], U32)
+        dy_w = [dy_first[:]] + [dy_rest[:, s, :] for s in range(PASSES - 1)]
         dy_s = sb("dy_s", [P, T], U8)
         wb_s_first = sb("wb_s_first", [P, 2 * PASSES, H], U8)
         wb_s_rest = sb("wb_s_rest", [P, 2 * PASSES, H], U8)
@@ -62,8 +62,6 @@ def tile_moe_adb_none_kernel(
         make_identity(nc, ident[:])
         for plane in (wb_s_first, wb_s_rest, wa_s, wt_s):
             nc.vector.memset(plane[:].bitcast(I32), 0)
-        dy_rest = sb("dy_rest", [P, PASSES - 1, T], U32)
-        dy_w = [dy_first[:]] + [dy_rest[:, s, :] for s in range(PASSES - 1)]
 
         dy_hbm = dy_words.rearrange("s p t d -> p s (t d)").bitcast(I32)
         wb_hbm = wbt_words.rearrange("e s p i d -> p (e s) (i d)").bitcast(I32)
@@ -77,14 +75,21 @@ def tile_moe_adb_none_kernel(
         def load_dy_scales(queue, q):
             queue.dma_start(out=dy_s[32 * q:32 * q + 4 * PASSES, :].bitcast(I32), in_=dys_hbm[:, 4 * q:4 * q + 4, :])
 
-        def load_scales(plane, row, hbm):
-            for r in range(4):
+        def load_scales(plane, row, hbm, rows=(0, 1, 2, 3)):
+            for r in rows:
                 nc.sync.dma_start(out=plane[row + r:P:32, :, :].bitcast(I32), in_=hbm[r:16:4])
 
-        def load_words(dst, hbm):
-            view = dst.rearrange("p (a c) -> p a c", a=hbm.shape[1])
-            nc.sync.dma_start(out=view.bitcast(I32), in_=hbm)
-            return [view[:, a, :] for a in range(hbm.shape[1])]
+        def load_words(name, hbm):
+            dst = sb(name, [P, hbm.shape[1], hbm.shape[2]], U32)
+            nc.sync.dma_start(out=dst[:].bitcast(I32), in_=hbm)
+            return [dst[:, a, :] for a in range(hbm.shape[1])]
+
+        wb_w = {}
+
+        def load_wb(planes):
+            got = load_words("wb%d" % planes.start, wb_hbm[:, planes, :])
+            for a, view in zip(range(planes.start, planes.stop, planes.step), got):
+                wb_w[divmod(a, PASSES)] = view
 
         nc.sync.dma_start(offs_sb[:], offs)
         nc.sync.dma_start(out=dy_first[:].bitcast(I32), in_=dy_hbm[:, 0, :])
@@ -92,19 +97,21 @@ def tile_moe_adb_none_kernel(
         for q in range(2):
             load_dy_scales(nc.scalar, q)
             load_dy_scales(nc.sync, q + 2)
-
-        wb_columns = E * PASSES * H
-        weights = sb("weights", [P, wb_columns + E * K + PASSES * K], U32)
-        wb_w = []
-        for n, (a0, a1) in enumerate(WB_LOADS):
-            wb_w.extend(load_words(weights[:, a0 * H:a1 * H], wb_hbm[:, a0:a1, :]))
-            if n == 0:
-                nc.sync.dma_start(out=gate_rows[0:S // P, :], in_=gate.rearrange("r (c p) -> (r c) p", p=P)[0:S // P, :])
-                load_scales(wb_s_first, WB_FIRST_ROW, wbs_hbm[:, 0:2 * PASSES, :])
-            if n == 1:
-                load_scales(wb_s_rest, WB_REST_ROW, wbs_hbm[:, 2 * PASSES:E * PASSES, :])
+        nc.sync.dma_start(out=gate_rows[0:S // P, :], in_=gate.rearrange("r (c p) -> (r c) p", p=P)[0:S // P, :])
+        load_wb(slice(0, 3, 1))
+        load_scales(wb_s_first, WB_FIRST_ROW, wbs_hbm[:, 0:2 * PASSES, :])
+        load_wb(slice(3, 6, 1))
+        load_scales(wb_s_rest, WB_REST_ROW, wbs_hbm[:, 2 * PASSES:E * PASSES, :])
+        for a0, a1 in ((6, 7), (7, 9), (9, 11), (11, 12)):
+            load_wb(slice(a0, a1, 1))
         wb_s = ([wb_s_first[WB_FIRST_ROW:P, a, :] for a in range(2 * PASSES)]
                 + [wb_s_rest[WB_REST_ROW:P, a, :] for a in range(2 * PASSES)])
+        load_scales(wa_s, WA_ROW, was_hbm)
+        wa_w = load_words("wa", wa_hbm)
+        load_scales(wt_s, WT_ROW, wts_hbm)
+        wt_w = load_words("wt", wt_hbm)
+        nc.sync.dma_start(pos_sb[0][:], pos1)
+        nc.sync.dma_start(pos_sb[1][:], pos2)
 
         gate_turned = bank(GATE_BANK, [P, P])
         nc.tensor.transpose(gate_turned[:], gate_rows[:], ident[:])
@@ -112,107 +119,118 @@ def tile_moe_adb_none_kernel(
 
         got_bytes, got_words = {}, {}
 
-        def gather_bytes(dst, j0):
-            size = dst.shape[1]
-            nc.vector.tensor_copy(dst, dy_s[:].indirect(offs_sb[:, j0 // 16:(j0 + size) // 16]))
-            for j in range(j0, j0 + size, P):
-                got_bytes[j] = dst[:, j - j0:j - j0 + P]
+        def offsets(m, tiles):
+            return offs_sb[:, m * P // 16:(m + tiles) * P // 16]
 
-        def gather_words(dst, j0, s):
-            size = dst.shape[1]
-            nc.vector.tensor_copy(dst, dy_w[s].indirect(offs_sb[:, j0 // 16:(j0 + size) // 16]))
-            for j in range(j0, j0 + size, P):
-                got_words[(j, s)] = dst[:, j - j0:j - j0 + P]
+        def gather_bytes(m, tiles, room=None):
+            dst = sb("bytes%d" % m, [P, tiles, P], U8, room)
+            for n in range(0, tiles, 2):
+                nc.vector.tensor_copy(dst[:, n:n + 2, :].rearrange("p m j -> p (m j)"), dy_s[:].indirect(offsets(m + n, 2)))
+            for n in range(tiles):
+                got_bytes[m + n] = dst[:, n, :]
+            return dst[:].rearrange("p m j -> p (m j)")
 
-        def gather_group(name, pieces):
-            group = sb(name + "_sb", [P, sum(size for j0, size, s in pieces)], U32, name)
-            at = 0
-            for j0, size, s in pieces:
-                gather_words(group[:, at:at + size], j0, s)
-                at += size
+        def gather_group(name, pieces, room=None):
+            gather_into(sb(name, [P, P * sum(tiles for m, tiles, s in pieces)], U32, room), 0, pieces)
 
-        early_words = sb("early_words", [P, C], U32)
-        gather_words(early_words[:], P, 0)
-        gather_words(sb("tile0_pass0", [P, P], U32, "late_bytes")[:], 0, 0)
-        gather_words(sb("adapter0_pass1", [P, C], U32, "late_words")[:], 0, 1)
-        gather_words(sb("tile0_pass2", [P, P], U32)[:], 0, 2)
-        first_bytes = sb("first_bytes", [P, C], U8)
-        gather_bytes(first_bytes[:], 0)
-        gather_bytes(sb("second_bytes", [P, C], U8)[:], C)
-        gather_group("second_words", ((P, P, 2), (C + P, P, 0), (C, C, 1), (C, C, 2), (2 * C, 3 * P, 0)))
+        def gather_into(group, at, pieces):
+            for m, tiles, s in pieces:
+                nc.vector.tensor_copy(group[:, at:at + tiles * P], dy_w[s].indirect(offsets(m, tiles)))
+                for n in range(tiles):
+                    got_words[(m + n, s)] = group[:, at:at + P]
+                    at += P
 
-        warm = bank(WARM_BANK, [P, C])
-        for n in range(WARM_PASSES):
-            nc.tensor.matmul_mx(out=warm[:], lhsT=early_words[:, 0:P].bitcast(X4), lhsT_scale=first_bytes[:, 0:P],
-                                rhs=early_words[:, 0:C].bitcast(X4), rhs_scale=first_bytes[:], start=True, stop=True)
+        accs = {}
 
-        load_scales(wa_s, WA_ROW, was_hbm)
-        wa_w = load_words(weights[:, wb_columns:wb_columns + E * K], wa_hbm)
-        load_scales(wt_s, WT_ROW, wts_hbm)
-        wt_w = load_words(weights[:, wb_columns + E * K:wb_columns + E * K + PASSES * K], wt_hbm)
-        nc.sync.dma_start(pos_sb[0][:], pos1)
-        nc.sync.dma_start(pos_sb[1][:], pos2)
+        def first_pass(m, s):
+            if s == 0:
+                accs[m] = [bank(b, [P, H // len(TILE_BANKS[m])]) for b in TILE_BANKS[m]]
+            e = m // 2
+            for n, acc in enumerate(accs[m]):
+                width = acc.shape[1]
+                cols = slice(n * width, (n + 1) * width)
+                nc.tensor.matmul_mx(
+                    out=acc[:],
+                    lhsT=got_words[(m, s)].bitcast(X4),
+                    lhsT_scale=got_bytes[m][4 * s:P, :],
+                    rhs=wb_w[(e, s)][:, cols].bitcast(X4),
+                    rhs_scale=wb_s[e * PASSES + s][:, cols],
+                    start=(s == 0), stop=(s == PASSES - 1),
+                )
 
-        def first_product(j):
-            e = j // C
-            m = j // P
-            dh = sb("dh%d" % m, [P, 2, P, 2], BF16)
-            banks = LAST_TILE_BANKS if j == S - P else (m,)
-            width = H // len(banks)
-            accs = [bank(b, [P, width]) for b in banks]
-            for s in range(PASSES):
-                for n, acc in enumerate(accs):
-                    cols = slice(n * width, (n + 1) * width)
-                    nc.tensor.matmul_mx(
-                        out=acc[:],
-                        lhsT=got_words[(j, s)].bitcast(X4),
-                        lhsT_scale=got_bytes[j][4 * s:P, :],
-                        rhs=wb_w[e * PASSES + s][:, cols].bitcast(X4),
-                        rhs_scale=wb_s[e * PASSES + s][:, cols],
-                        start=(s == 0), stop=(s == PASSES - 1),
-                    )
-            for n, acc in enumerate(accs):
-                dst = dh[:, :, n * width // 4:(n + 1) * width // 4, :]
+        dhs = {}
+
+        def empty(m):
+            dhs[m] = sb("dh%d" % m, [P, 2, P, 2], BF16)
+            for n, acc in enumerate(accs[m]):
+                part = acc.shape[1] // 4
+                dst = dhs[m][:, :, n * part:(n + 1) * part, :]
                 src = acc[:].rearrange("j (p u v) -> j u p v", u=2, v=2)
                 if n == 0:
                     nc.scalar.activation(dst, src, COPY, scale=gate_cols[:, m:m + 1])
                 else:
                     nc.vector.tensor_scalar(dst, src, gate_cols[:, m:m + 1], None, MULT)
-            return dh
 
-        def turn(n, tiles):
-            turned = bank(TURN_BANKS[n], [P, 4, P])
-            for m, dh in enumerate(tiles):
-                pairs = dh[:].rearrange("j u p v -> j (u p v)").bitcast(F32)
-                for u in range(2):
-                    nc.tensor.transpose(turned[:, 2 * m + u, :], pairs[:, u * P:(u + 1) * P], ident[:])
-            dht = sb("dht%d" % n, [P, len(tiles), P, 2], F32)
-            copy = nc.vector.tensor_copy if n == len(TURNS) - 1 else nc.scalar.copy
-            copy(dht[:], turned[:, 0:2 * len(tiles), :].rearrange("p (m u) j -> p m j u", u=2))
-            return dht
-
-        dhs = [first_product(0), first_product(P)]
-
-        late_bytes = sb("late_bytes_sb", [P, 2 * C], U8, "late_bytes")
-        gather_bytes(late_bytes[:, 0:3 * P], 2 * C)
-        gather_bytes(late_bytes[:, 3 * P:4 * P], S - P)
-        gather_group("late_words", ((2 * C, C, 1), (2 * C, C, 2), (S - P, P, 0),
-                                    (3 * C, C, 1), (3 * C, P, 2), (S - P, P, 2)))
-
-        dhts = []
-        for j in range(2 * P, S, P):
-            dhs.append(first_product(j))
-            while len(dhts) < len(TURNS) - 1 and sum(TURNS[len(dhts)]) <= j:
-                j0, size = TURNS[len(dhts)]
-                dhts.append(turn(len(dhts), dhs[j0 // P:(j0 + size) // P]))
-        dhts.append(turn(len(dhts), dhs[-1:]))
-
-        dx = [sb("dx%d" % h, [P, S], F32) for h in range(2)]
         dh_codes = sb("dh_codes", [P, S], U32)
         dh_scales = sb("dh_scales", [P, S], U8)
-        for n, (j0, size) in enumerate(TURNS):
-            nc.vector.quantize_mx(out=dh_codes[:, j0:j0 + size].bitcast(X4), scales=dh_scales[:, j0:j0 + size],
+        dhts = {}
+
+        def turn(n, copy):
+            m0, tiles, b = TURNS[n]
+            turned = bank(b, [P, 2 * tiles, P])
+            for m in range(tiles):
+                pairs = dhs[m0 + m][:].rearrange("j u p v -> j (u p v)").bitcast(F32)
+                for u in range(2):
+                    nc.tensor.transpose(turned[:, 2 * m + u, :], pairs[:, u * P:(u + 1) * P], ident[:])
+            dhts[n] = sb("dht%d" % n, [P, tiles, P, 2], F32)
+            copy(dhts[n][:], turned[:].rearrange("p (m u) j -> p m j u", u=2))
+
+        def quantise(n):
+            m0, tiles, b = TURNS[n]
+            cols = slice(m0 * P, (m0 + tiles) * P)
+            nc.vector.quantize_mx(out=dh_codes[:, cols].bitcast(X4), scales=dh_scales[:, cols],
                                   in_=dhts[n][:].rearrange("p m j u -> p (m j u)").bitcast(BF16))
+
+        gather_group("words0", ((0, 1, 0),), "late_bytes")
+        gather_group("words1", ((1, 1, 0),), "late_words")
+        warm_words = sb("words23", [P, C], U32)
+        gather_into(warm_words, 0, ((2, 2, 0),))
+        warm_bytes = gather_bytes(0, 2)
+        gather_bytes(2, 2)
+        gather_group("second_words_sb", ((0, 2, 1), (0, 2, 2), (2, 2, 1), (2, 2, 2)), "second_words")
+
+        warm = bank(WARM_BANK, [P, C])
+        for n in range(WARM_PASSES):
+            nc.tensor.matmul_mx(out=warm[:], lhsT=got_words[(2, 0)].bitcast(X4), lhsT_scale=got_bytes[0],
+                                rhs=warm_words[:].bitcast(X4), rhs_scale=warm_bytes, start=True, stop=True)
+
+        def product(m):
+            for s in range(PASSES):
+                first_pass(m, s)
+            empty(m)
+
+        product(0)
+        product(1)
+        gather_bytes(4, 4, "late_bytes")
+        gather_group("late_words_sb", ((4, 2, 0), (4, 2, 1), (4, 2, 2), (6, 2, 0), (6, 2, 1), (6, 1, 2), (7, 1, 2)),
+                     "late_words")
+        product(2)
+        product(3)
+        turn(0, nc.scalar.copy)
+        product(4)
+        product(5)
+        turn(1, nc.scalar.copy)
+        product(6)
+        product(7)
+        quantise(0)
+        quantise(1)
+        turn(2, nc.scalar.copy)
+        turn(3, nc.vector.tensor_copy)
+        turn(4, nc.scalar.copy)
+        for n in (2, 3, 4):
+            quantise(n)
+
+        dx = [sb("dx%d" % h, [P, S], F32) for h in range(2)]
 
         def second_product(h, first, sizes, b):
             acc = bank(b, [P, sum(sizes)])
@@ -241,14 +259,14 @@ def tile_moe_adb_none_kernel(
                 )
             return acc
 
-        for first, sizes, banks in ((0, (C, C), (2, 3)), (2 * C, (C, P), (0, 6)), (S - P, (P,), LAST_TILE_BANKS)):
+        for first, sizes, banks in ((0, (C, C), (2, 4)), (2 * C, (C, P), (6, 1)), (S - P, (P,), (7, 3))):
             for h in range(2):
                 second_product(h, first, sizes, banks[h])
 
         base_first = sb("base_first", [P, C], F32)
-        nc.scalar.copy(base_first[:], frozen(0, 0, C, TURN_BANKS[-2])[:])
-        base_second = frozen(0, C, C, TURN_BANKS[-1])
-        base_lower = frozen(1, 0, T, LAST_TILE_BANKS[0])
+        nc.scalar.copy(base_first[:], frozen(0, 0, C, 0)[:])
+        base_second = frozen(0, C, C, 5)
+        base_lower = frozen(1, 0, T, 2)
 
         def picked(h, r, t0, size):
             return dx[h][:].indirect(pos_sb[r][:, t0 // 16:(t0 + size) // 16])

@@ -108,8 +108,8 @@ def tile_moe_adb_none_kernel(
                 + [wb_s_rest[WB_REST_ROW:P, a, :] for a in range(2 * PASSES)])
         load_scales(wa_s, WA_ROW, was_hbm)
         wa_w = load_words("wa", wa_hbm)
-        load_scales(wt_s, WT_ROW, wts_hbm)
         wt_w = load_words("wt", wt_hbm)
+        load_scales(wt_s, WT_ROW, wts_hbm)
         nc.sync.dma_start(pos_sb[0][:], pos1)
         nc.sync.dma_start(pos_sb[1][:], pos2)
 

@@ -21,10 +21,10 @@ ADD = mybir.AluOpType.add
 MULT = mybir.AluOpType.mult
 
 WB_FIRST_ROW, WB_REST_ROW, WT_ROW, WA_ROW = 0, 4, 8, 12
-TILE_BANKS = ((0,), (1,), (2,), (3,), (4,), (5,), (6, 1), (7, 3))
+TILE_BANKS = ((0,), (1,), (2, 6), (3,), (4, 0), (5,), (6, 1), (7, 3))
 TURNS = ((0, 2, 2), (2, 2, 4), (4, 2, 6), (6, 1, 0), (7, 1, 5))
 GATE_BANK, WARM_BANK = 5, 5
-WARM_PASSES = 4
+WARM_PASSES = 6
 
 
 def tile_moe_adb_none_kernel(
@@ -50,7 +50,8 @@ def tile_moe_adb_none_kernel(
         dy_w = [dy_first[:]] + [dy_rest[:, s, :] for s in range(PASSES - 1)]
         dy_s = sb("dy_s", [P, T], U8)
         wb_s_first = sb("wb_s_first", [P, 2 * PASSES, H], U8)
-        wb_s_rest = sb("wb_s_rest", [P, 2 * PASSES, H], U8)
+        wb_s_packed = sb("wb_s_packed", [P, H], U8)
+        wb_s_rest = sb("wb_s_rest", [P, 2, H], U8)
         wa_s = sb("wa_s", [P, E, K], U8)
         wt_s = sb("wt_s", [P, PASSES, K], U8)
         gate_rows = sb("gate_rows", [P, P], F32, "second_words")
@@ -60,7 +61,7 @@ def tile_moe_adb_none_kernel(
         nc.gpsimd.memset(dy_s[:].bitcast(I32), 0)
         nc.gpsimd.memset(gate_rows[:], 0.0)
         make_identity(nc, ident[:])
-        for plane in (wb_s_first, wb_s_rest, wa_s, wt_s):
+        for plane in (wb_s_first, wb_s_packed, wb_s_rest, wa_s, wt_s):
             nc.vector.memset(plane[:].bitcast(I32), 0)
 
         dy_hbm = dy_words.rearrange("s p t d -> p s (t d)").bitcast(I32)
@@ -69,6 +70,7 @@ def tile_moe_adb_none_kernel(
         wt_hbm = wt_words.rearrange("s p k d -> p s (k d)").bitcast(I32)
         dys_hbm = dy_scales.bitcast(I32)
         wbs_hbm = wbt_scales.bitcast(I32).rearrange("e s b i -> b (e s) i")
+        wbs_planes = wbt_scales.bitcast(I32).rearrange("e s b i -> (e s) b i")
         was_hbm = wat_scales.bitcast(I32).rearrange("e s b k -> b (e s) k")
         wts_hbm = wt_scales.bitcast(I32).rearrange("s b k -> b s k")
 
@@ -78,6 +80,10 @@ def tile_moe_adb_none_kernel(
         def load_scales(plane, row, hbm, rows=(0, 1, 2, 3)):
             for r in rows:
                 nc.sync.dma_start(out=plane[row + r:P:32, :, :].bitcast(I32), in_=hbm[r:16:4])
+
+        def load_packed(plane, hbm):
+            for q in range(4):
+                nc.sync.dma_start(out=plane[32 * q:32 * q + 16, :].bitcast(I32), in_=hbm[:, 4 * q:4 * q + 4, :])
 
         def load_words(name, hbm):
             dst = sb(name, [P, hbm.shape[1], hbm.shape[2]], U32)
@@ -100,14 +106,17 @@ def tile_moe_adb_none_kernel(
         nc.sync.dma_start(out=gate_rows[0:S // P, :], in_=gate.rearrange("r (c p) -> (r c) p", p=P)[0:S // P, :])
         load_wb(slice(0, 3, 1))
         load_scales(wb_s_first, WB_FIRST_ROW, wbs_hbm[:, 0:2 * PASSES, :])
-        load_wb(slice(3, 6, 1))
-        load_scales(wb_s_rest, WB_REST_ROW, wbs_hbm[:, 2 * PASSES:E * PASSES, :])
-        for a0, a1 in ((6, 7), (7, 9), (9, 11), (11, 12)):
+        load_wb(slice(3, 4, 1))
+        load_wb(slice(4, 6, 1))
+        load_packed(wb_s_packed, wbs_planes[6:10])
+        load_wb(slice(6, 9, 1))
+        load_scales(wb_s_rest, WB_REST_ROW, wbs_hbm[:, 10:12, :])
+        for a0, a1 in ((9, 11), (11, 12)):
             load_wb(slice(a0, a1, 1))
         wb_s = ([wb_s_first[WB_FIRST_ROW:P, a, :] for a in range(2 * PASSES)]
-                + [wb_s_rest[WB_REST_ROW:P, a, :] for a in range(2 * PASSES)])
+                + [wb_s_packed[4 * a:P, :] for a in range(4)] + [wb_s_rest[WB_REST_ROW:P, a, :] for a in range(2)])
         load_scales(wa_s, WA_ROW, was_hbm)
-        wa_w = load_words("wa", wa_hbm)
+        wa_w = load_words("wa_first", wa_hbm[:, 0:2, :]) + load_words("wa_rest", wa_hbm[:, 2:E, :])
         wt_w = load_words("wt", wt_hbm)
         load_scales(wt_s, WT_ROW, wts_hbm)
         nc.sync.dma_start(pos_sb[0][:], pos1)
@@ -166,7 +175,7 @@ def tile_moe_adb_none_kernel(
                 part = acc.shape[1] // 4
                 dst = dhs[m][:, :, n * part:(n + 1) * part, :]
                 src = acc[:].rearrange("j (p u v) -> j u p v", u=2, v=2)
-                if n == 0:
+                if n == 0 or m < 6:
                     nc.scalar.activation(dst, src, COPY, scale=gate_cols[:, m:m + 1])
                 else:
                     nc.vector.tensor_scalar(dst, src, gate_cols[:, m:m + 1], None, MULT)
@@ -271,9 +280,9 @@ def tile_moe_adb_none_kernel(
         def picked(h, r, t0, size):
             return dx[h][:].indirect(pos_sb[r][:, t0 // 16:(t0 + size) // 16])
 
-        def fetch(h, r, t0):
-            got = sb("got%d_%d_%d" % (h, r, t0), [P, C], F32)
-            nc.scalar.activation(got[:], picked(h, r, t0, C), COPY)
+        def fetch(h, r, t0, size=C):
+            got = sb("got%d_%d_%d" % (h, r, t0), [P, size], F32)
+            nc.scalar.activation(got[:], picked(h, r, t0, size), COPY)
             return got[:]
 
         def add(name, h, t0, size, in0, in1):
@@ -289,6 +298,7 @@ def tile_moe_adb_none_kernel(
         for t0, part in zip(pieces, fused):
             finish(0, t0, P, picked(0, 1, t0, P), part)
         finish(0, C, C, picked(0, 1, C, C), add("part", 0, C, C, base_second[:], fetch(0, 0, C)))
-        for t0 in (0, C):
-            part = add("part", 1, t0, C, base_lower[:, t0:t0 + C], fetch(1, 0, t0))
-            finish(1, t0, C, fetch(1, 1, t0), part)
+        finish(1, 0, C, fetch(1, 1, 0), add("part", 1, 0, C, base_lower[:, 0:C], fetch(1, 0, 0)))
+        part = add("part", 1, C, C, base_lower[:, C:T], fetch(1, 0, C))
+        for t0 in (C, C + P):
+            finish(1, t0, P, fetch(1, 1, t0, P), part[:, t0 - C:t0 - C + P])

@@ -21,10 +21,10 @@ ADD = mybir.AluOpType.add
 MULT = mybir.AluOpType.mult
 
 WB_FIRST_ROW, WB_REST_ROW, WT_ROW, WA_ROW = 0, 4, 8, 12
-TILE_BANKS = ((0,), (1,), (2, 6), (3,), (4, 0), (5,), (6, 1), (7, 3))
-TURNS = ((0, 2, 2), (2, 2, 4), (4, 2, 6), (6, 1, 0), (7, 1, 5))
+TILE_BANKS = ((0,), (1,), (2, 6), (3,), (4,), (5,), (6, 1), (7, 3))
+TURNS = ((0, 2, 2), (2, 2, 2), (4, 2, 6), (6, 1, 0), (7, 1, 5))
 GATE_BANK, WARM_BANK = 5, 5
-WARM_PASSES = 6
+WARM_PASSES = 5
 
 
 def tile_moe_adb_none_kernel(
@@ -49,9 +49,8 @@ def tile_moe_adb_none_kernel(
         dy_rest = sb("dy_rest", [P, PASSES - 1, T], U32)
         dy_w = [dy_first[:]] + [dy_rest[:, s, :] for s in range(PASSES - 1)]
         dy_s = sb("dy_s", [P, T], U8)
-        wb_s_first = sb("wb_s_first", [P, 2 * PASSES, H], U8)
-        wb_s_packed = sb("wb_s_packed", [P, H], U8)
-        wb_s_rest = sb("wb_s_rest", [P, 2, H], U8)
+        wb_s_packed = [sb("wb_s_packed%d" % g, [P, H], U8) for g in range(2)]
+        wb_s_rest = sb("wb_s_rest", [P, 4, H], U8)
         wa_s = sb("wa_s", [P, E, K], U8)
         wt_s = sb("wt_s", [P, PASSES, K], U8)
         gate_rows = sb("gate_rows", [P, P], F32, "second_words")
@@ -61,7 +60,7 @@ def tile_moe_adb_none_kernel(
         nc.gpsimd.memset(dy_s[:].bitcast(I32), 0)
         nc.gpsimd.memset(gate_rows[:], 0.0)
         make_identity(nc, ident[:])
-        for plane in (wb_s_first, wb_s_packed, wb_s_rest, wa_s, wt_s):
+        for plane in (wt_s, wb_s_packed[0], wb_s_packed[1], wb_s_rest, wa_s):
             nc.vector.memset(plane[:].bitcast(I32), 0)
 
         dy_hbm = dy_words.rearrange("s p t d -> p s (t d)").bitcast(I32)
@@ -105,20 +104,20 @@ def tile_moe_adb_none_kernel(
             load_dy_scales(nc.sync, q + 2)
         nc.sync.dma_start(out=gate_rows[0:S // P, :], in_=gate.rearrange("r (c p) -> (r c) p", p=P)[0:S // P, :])
         load_wb(slice(0, 3, 1))
-        load_scales(wb_s_first, WB_FIRST_ROW, wbs_hbm[:, 0:2 * PASSES, :])
-        load_wb(slice(3, 4, 1))
-        load_wb(slice(4, 6, 1))
-        load_packed(wb_s_packed, wbs_planes[6:10])
+        load_scales(wt_s, WT_ROW, wts_hbm, (0, 1))
+        load_packed(wb_s_packed[0], wbs_planes[0:4])
+        load_wb(slice(3, 6, 1))
+        load_packed(wb_s_packed[1], wbs_planes[4:8])
         load_wb(slice(6, 9, 1))
-        load_scales(wb_s_rest, WB_REST_ROW, wbs_hbm[:, 10:12, :])
+        load_scales(wb_s_rest, WB_REST_ROW, wbs_hbm[:, 8:12, :])
         for a0, a1 in ((9, 11), (11, 12)):
             load_wb(slice(a0, a1, 1))
-        wb_s = ([wb_s_first[WB_FIRST_ROW:P, a, :] for a in range(2 * PASSES)]
-                + [wb_s_packed[4 * a:P, :] for a in range(4)] + [wb_s_rest[WB_REST_ROW:P, a, :] for a in range(2)])
+        wb_s = ([wb_s_packed[a // 4][4 * (a % 4):P, :] for a in range(8)]
+                + [wb_s_rest[WB_REST_ROW:P, a, :] for a in range(4)])
         load_scales(wa_s, WA_ROW, was_hbm)
         wa_w = load_words("wa_first", wa_hbm[:, 0:2, :]) + load_words("wa_rest", wa_hbm[:, 2:E, :])
         wt_w = load_words("wt", wt_hbm)
-        load_scales(wt_s, WT_ROW, wts_hbm)
+        load_scales(wt_s, WT_ROW, wts_hbm, (2, 3))
         nc.sync.dma_start(pos_sb[0][:], pos1)
         nc.sync.dma_start(pos_sb[1][:], pos2)
 

from contextlib import ExitStack

import concourse.mybir as mybir
from concourse.masks import make_identity

K, T, E, C, H, N = 256, 512, 4, 256, 512, 1536
S = E * C
P = 128
PASSES = N // 512
FLOPS = 2 * N * K * T + 2 * N * H * S + 2 * H * K * S

F32 = mybir.dt.float32
BF16 = mybir.dt.bfloat16
I32 = mybir.dt.int32
U32 = mybir.dt.uint32
U16 = mybir.dt.uint16
U8 = mybir.dt.uint8
X4 = mybir.dt.float8_e4m3fn_x4
COPY = mybir.ActivationFunctionType.Copy
ADD = mybir.AluOpType.add
MULT = mybir.AluOpType.mult

WB_FIRST_ROW, WB_REST_ROW, WT_ROW, WA_ROW = 0, 4, 8, 12
TILE_BANKS = ((0,), (1,), (2, 6), (3,), (4,), (5,), (6, 1), (7, 3))
TURNS = ((0, 2, 2), (2, 2, 2), (4, 2, 6), (6, 1, 0), (7, 1, 5))
GATE_BANK, WARM_BANK = 5, 5
WARM_PASSES = 5


def tile_moe_adb_none_kernel(
    tc, dy_words, dy_scales, wt_words, wt_scales, wbt_words, wbt_scales, wat_words, wat_scales,
    gate, offs, pos1, pos2, out,
):
    nc = tc.nc
    with ExitStack() as ctx:
        keep = ctx.enter_context(tc.tile_pool(name="keep", bufs=1))
        psum = ctx.enter_context(tc.psum_pool(name="psum", bufs=1))

        def sb(name, shape, dtype, room=None):
            return keep.tile(shape, dtype, name=name, tag=room or name, align_bytes=64)

        def bank(n, shape):
            return psum.tile(shape, F32, name="bank%d" % n, tag="bank%d" % n)

        offs_sb = keep.tile([P, S // 16], U16, name="offs_sb")
        pos_sb = [keep.tile([P, T // 16], U16, name="pos%d_sb" % r) for r in range(2)]

        dy_first = sb("dy_first", [P, T], U32)
        dy_rest = sb("dy_rest", [P, PASSES - 1, T], U32)
        dy_w = [dy_first[:]] + [dy_rest[:, s, :] for s in range(PASSES - 1)]
        dy_s = sb("dy_s", [P, T], U8)
        wb_s_packed = [sb("wb_s_packed%d" % g, [P, H], U8) for g in range(2)]
        wb_s_rest = sb("wb_s_rest", [P, 4, H], U8)
        wa_s = sb("wa_s", [P, E, K], U8)
        wt_s = sb("wt_s", [P, PASSES, K], U8)
        gate_rows = sb("gate_rows", [P, P], F32, "second_words")
        gate_cols = sb("gate_cols", [P, S // P], F32)
        ident = sb("ident", [P, P], F32)

        nc.gpsimd.memset(dy_s[:].bitcast(I32), 0)
        nc.gpsimd.memset(gate_rows[:], 0.0)
        make_identity(nc, ident[:])
        for plane in (wt_s, wb_s_packed[0], wb_s_packed[1], wb_s_rest, wa_s):
            nc.vector.memset(plane[:].bitcast(I32), 0)

        dy_hbm = dy_words.rearrange("s p t d -> p s (t d)").bitcast(I32)
        wb_hbm = wbt_words.rearrange("e s p i d -> p (e s) (i d)").bitcast(I32)
        wa_hbm = wat_words.rearrange("e s p k d -> p (e s) (k d)").bitcast(I32)
        wt_hbm = wt_words.rearrange("s p k d -> p s (k d)").bitcast(I32)
        dys_hbm = dy_scales.bitcast(I32)
        wbs_hbm = wbt_scales.bitcast(I32).rearrange("e s b i -> b (e s) i")
        wbs_planes = wbt_scales.bitcast(I32).rearrange("e s b i -> (e s) b i")
        was_hbm = wat_scales.bitcast(I32).rearrange("e s b k -> b (e s) k")
        wts_hbm = wt_scales.bitcast(I32).rearrange("s b k -> b s k")

        def load_dy_scales(queue, q):
            queue.dma_start(out=dy_s[32 * q:32 * q + 4 * PASSES, :].bitcast(I32), in_=dys_hbm[:, 4 * q:4 * q + 4, :])

        def load_scales(plane, row, hbm, rows=(0, 1, 2, 3)):
            for r in rows:
                nc.sync.dma_start(out=plane[row + r:P:32, :, :].bitcast(I32), in_=hbm[r:16:4])

        def load_packed(plane, hbm):
            for q in range(4):
                nc.sync.dma_start(out=plane[32 * q:32 * q + 16, :].bitcast(I32), in_=hbm[:, 4 * q:4 * q + 4, :])

        def load_words(name, hbm):
            dst = sb(name, [P, hbm.shape[1], hbm.shape[2]], U32)
            nc.sync.dma_start(out=dst[:].bitcast(I32), in_=hbm)
            return [dst[:, a, :] for a in range(hbm.shape[1])]

        wb_w = {}

        def load_wb(planes):
            got = load_words("wb%d" % planes.start, wb_hbm[:, planes, :])
            for a, view in zip(range(planes.start, planes.stop, planes.step), got):
                wb_w[divmod(a, PASSES)] = view

        nc.sync.dma_start(offs_sb[:], offs)
        nc.sync.dma_start(out=dy_first[:].bitcast(I32), in_=dy_hbm[:, 0, :])
        nc.sync.dma_start(out=dy_rest[:].bitcast(I32), in_=dy_hbm[:, 1:PASSES, :])
        for q in range(2):
            load_dy_scales(nc.scalar, q)
            load_dy_scales(nc.sync, q + 2)
        nc.sync.dma_start(out=gate_rows[0:S // P, :], in_=gate.rearrange("r (c p) -> (r c) p", p=P)[0:S // P, :])
        load_wb(slice(0, 3, 1))
        load_scales(wt_s, WT_ROW, wts_hbm, (0, 1))
        load_packed(wb_s_packed[0], wbs_planes[0:4])
        load_wb(slice(3, 6, 1))
        load_packed(wb_s_packed[1], wbs_planes[4:8])
        load_wb(slice(6, 9, 1))
        load_scales(wb_s_rest, WB_REST_ROW, wbs_hbm[:, 8:12, :])
        for a0, a1 in ((9, 11), (11, 12)):
            load_wb(slice(a0, a1, 1))
        wb_s = ([wb_s_packed[a // 4][4 * (a % 4):P, :] for a in range(8)]
                + [wb_s_rest[WB_REST_ROW:P, a, :] for a in range(4)])
        load_scales(wa_s, WA_ROW, was_hbm)
        wa_w = load_words("wa_first", wa_hbm[:, 0:2, :]) + load_words("wa_rest", wa_hbm[:, 2:E, :])
        wt_w = load_words("wt", wt_hbm)
        load_scales(wt_s, WT_ROW, wts_hbm, (2, 3))
        nc.sync.dma_start(pos_sb[0][:], pos1)
        nc.sync.dma_start(pos_sb[1][:], pos2)

        gate_turned = bank(GATE_BANK, [P, P])
        nc.tensor.transpose(gate_turned[:], gate_rows[:], ident[:])
        nc.scalar.activation(gate_cols[:], gate_turned[:, 0:S // P], COPY)

        got_bytes, got_words = {}, {}

        def offsets(m, tiles):
            return offs_sb[:, m * P // 16:(m + tiles) * P // 16]

        def gather_bytes(m, tiles, room=None):
            dst = sb("bytes%d" % m, [P, tiles, P], U8, room)
            for n in range(0, tiles, 2):
                nc.vector.tensor_copy(dst[:, n:n + 2, :].rearrange("p m j -> p (m j)"), dy_s[:].indirect(offsets(m + n, 2)))
            for n in range(tiles):
                got_bytes[m + n] = dst[:, n, :]
            return dst[:].rearrange("p m j -> p (m j)")

        def gather_group(name, pieces, room=None):
            gather_into(sb(name, [P, P * sum(tiles for m, tiles, s in pieces)], U32, room), 0, pieces)

        def gather_into(group, at, pieces):
            for m, tiles, s in pieces:
                nc.vector.tensor_copy(group[:, at:at + tiles * P], dy_w[s].indirect(offsets(m, tiles)))
                for n in range(tiles):
                    got_words[(m + n, s)] = group[:, at:at + P]
                    at += P

        accs = {}

        def first_pass(m, s):
            if s == 0:
                accs[m] = [bank(b, [P, H // len(TILE_BANKS[m])]) for b in TILE_BANKS[m]]
            e = m // 2
            for n, acc in enumerate(accs[m]):
                width = acc.shape[1]
                cols = slice(n * width, (n + 1) * width)
                nc.tensor.matmul_mx(
                    out=acc[:],
                    lhsT=got_words[(m, s)].bitcast(X4),
                    lhsT_scale=got_bytes[m][4 * s:P, :],
                    rhs=wb_w[(e, s)][:, cols].bitcast(X4),
                    rhs_scale=wb_s[e * PASSES + s][:, cols],
                    start=(s == 0), stop=(s == PASSES - 1),
                )

        dhs = {}

        def empty(m):
            dhs[m] = sb("dh%d" % m, [P, 2, P, 2], BF16)
            for n, acc in enumerate(accs[m]):
                part = acc.shape[1] // 4
                dst = dhs[m][:, :, n * part:(n + 1) * part, :]
                src = acc[:].rearrange("j (p u v) -> j u p v", u=2, v=2)
                if n == 0 or m < 6:
                    nc.scalar.activation(dst, src, COPY, scale=gate_cols[:, m:m + 1])
                else:
                    nc.vector.tensor_scalar(dst, src, gate_cols[:, m:m + 1], None, MULT)

        dh_codes = sb("dh_codes", [P, S], U32)
        dh_scales = sb("dh_scales", [P, S], U8)
        dhts = {}

        def turn(n, copy):
            m0, tiles, b = TURNS[n]
            turned = bank(b, [P, 2 * tiles, P])
            for m in range(tiles):
                pairs = dhs[m0 + m][:].rearrange("j u p v -> j (u p v)").bitcast(F32)
                for u in range(2):
                    nc.tensor.transpose(turned[:, 2 * m + u, :], pairs[:, u * P:(u + 1) * P], ident[:])
            dhts[n] = sb("dht%d" % n, [P, tiles, P, 2], F32)
            copy(dhts[n][:], turned[:].rearrange("p (m u) j -> p m j u", u=2))

        def quantise(n):
            m0, tiles, b = TURNS[n]
            cols = slice(m0 * P, (m0 + tiles) * P)
            nc.vector.quantize_mx(out=dh_codes[:, cols].bitcast(X4), scales=dh_scales[:, cols],
                                  in_=dhts[n][:].rearrange("p m j u -> p (m j u)").bitcast(BF16))

        gather_group("words0", ((0, 1, 0),), "late_bytes")
        gather_group("words1", ((1, 1, 0),), "late_words")
        warm_words = sb("words23", [P, C], U32)
        gather_into(warm_words, 0, ((2, 2, 0),))
        warm_bytes = gather_bytes(0, 2)
        gather_bytes(2, 2)
        gather_group("second_words_sb", ((0, 2, 1), (0, 2, 2), (2, 2, 1), (2, 2, 2)), "second_words")

        warm = bank(WARM_BANK, [P, C])
        for n in range(WARM_PASSES):
            nc.tensor.matmul_mx(out=warm[:], lhsT=got_words[(2, 0)].bitcast(X4), lhsT_scale=got_bytes[0],
                                rhs=warm_words[:].bitcast(X4), rhs_scale=warm_bytes, start=True, stop=True)

        def product(m):
            for s in range(PASSES):
                first_pass(m, s)
            empty(m)

        product(0)
        product(1)
        gather_bytes(4, 4, "late_bytes")
        gather_group("late_words_sb", ((4, 2, 0), (4, 2, 1), (4, 2, 2), (6, 2, 0), (6, 2, 1), (6, 1, 2), (7, 1, 2)),
                     "late_words")
        product(2)
        product(3)
        turn(0, nc.scalar.copy)
        product(4)
        product(5)
        turn(1, nc.scalar.copy)
        product(6)
        product(7)
        quantise(0)
        quantise(1)
        turn(2, nc.scalar.copy)
        turn(3, nc.vector.tensor_copy)
        turn(4, nc.scalar.copy)
        for n in (2, 3, 4):
            quantise(n)

        dx = [sb("dx%d" % h, [P, S], F32) for h in range(2)]

        def second_product(h, first, sizes, b):
            acc = bank(b, [P, sum(sizes)])
            j0 = first
            for size in sizes:
                nc.tensor.matmul_mx(
                    out=acc[:, j0 - first:j0 - first + size],
                    lhsT=wa_w[j0 // C][:, h * P:(h + 1) * P].bitcast(X4),
                    lhsT_scale=wa_s[WA_ROW:P, j0 // C, h * P:(h + 1) * P],
                    rhs=dh_codes[:, j0:j0 + size].bitcast(X4), rhs_scale=dh_scales[:, j0:j0 + size],
                    start=True, stop=True,
                )
                j0 += size
            copy = nc.vector.tensor_copy if h else nc.scalar.copy
            copy(dx[h][:, first:j0], acc[:])

        def frozen(h, t0, size, b):
            acc = bank(b, [P, size])
            for s in range(PASSES):
                nc.tensor.matmul_mx(
                    out=acc[:],
                    lhsT=wt_w[s][:, h * P:(h + 1) * P].bitcast(X4),
                    lhsT_scale=wt_s[WT_ROW:P, s, h * P:(h + 1) * P],
                    rhs=dy_w[s][:, t0:t0 + size].bitcast(X4), rhs_scale=dy_s[4 * s:P, t0:t0 + size],
                    start=(s == 0), stop=(s == PASSES - 1),
                )
            return acc

        for first, sizes, banks in ((0, (C, C), (2, 4)), (2 * C, (C, P), (6, 1)), (S - P, (P,), (7, 3))):
            for h in range(2):
                second_product(h, first, sizes, banks[h])

        base_first = sb("base_first", [P, C], F32)
        nc.scalar.copy(base_first[:], frozen(0, 0, C, 0)[:])
        base_second = frozen(0, C, C, 5)
        base_lower = frozen(1, 0, T, 2)

        def picked(h, r, t0, size):
            return dx[h][:].indirect(pos_sb[r][:, t0 // 16:(t0 + size) // 16])

        def fetch(h, r, t0, size=C):
            got = sb("got%d_%d_%d" % (h, r, t0), [P, size], F32)
            nc.scalar.activation(got[:], picked(h, r, t0, size), COPY)
            return got[:]

        def add(name, h, t0, size, in0, in1):
            result = sb("%s%d_%d" % (name, h, t0), [P, size], F32)
            nc.vector.tensor_tensor(result[:], in0, in1, ADD)
            return result[:]

        def finish(h, t0, size, second, part):
            nc.sync.dma_start(out=out[h * P:(h + 1) * P, t0:t0 + size], in_=add("total", h, t0, size, second, part))

        pieces = (0, P)
        fused = [add("part", 0, t0, P, picked(0, 0, t0, P), base_first[:, t0:t0 + P]) for t0 in pieces]
        for t0, part in zip(pieces, fused):
            finish(0, t0, P, picked(0, 1, t0, P), part)
        finish(0, C, C, picked(0, 1, C, C), add("part", 0, C, C, base_second[:], fetch(0, 0, C)))
        finish(1, 0, C, fetch(1, 1, 0), add("part", 1, 0, C, base_lower[:, 0:C], fetch(1, 0, 0)))
        part = add("part", 1, C, C, base_lower[:, C:T], fetch(1, 0, C))
        for t0 in (C, C + P):
            finish(1, t0, P, fetch(1, 1, t0, P), part[:, t0 - C:t0 - C + P])
